import numpy as np
import ml_dtypes


def mxq(x, axis, fmt="e4m3"):
    dtype, down = {"e4m3": (ml_dtypes.float8_e4m3fn, 7), "e5m2": (ml_dtypes.float8_e5m2, 14)}[fmt]
    v = np.moveaxis(np.asarray(x, np.float32).astype(ml_dtypes.bfloat16).astype(np.float64), axis, -1)
    blocks = v.reshape(v.shape[:-1] + (-1, 32))
    amax = np.abs(blocks).max(-1, keepdims=True)
    byte = np.maximum(np.where(amax > 0, np.frexp(amax)[1] - 1 + 127, 0) - down, 1)
    scale = np.exp2(byte - 127.0)
    codes = (blocks / scale).astype(np.float32).astype(dtype).astype(np.float64)
    return np.moveaxis((codes * scale).reshape(v.shape), -1, axis)


WIDE = False


def mx_kscale(k):
    if not WIDE:
        return np.ones(k)
    levels = np.array([10, -10, 5, -5, 0])
    if k % 512:
        return np.exp2(np.random.permutation(np.resize(levels, k // 32))).repeat(32)
    a = np.empty((k // 512, 16))
    for p in range(k // 512):
        a[p, :8] = np.random.permutation(np.resize(levels, 8))
        for g in range(8):
            far = levels[np.abs(levels - a[p, g]) >= 10]
            a[p, g + 8] = far[np.random.randint(len(far))]
    return np.exp2(a.ravel()).repeat(32)


def f64(x):
    return np.asarray(x).astype(np.float64)


def striped(idx):
    return np.tile(idx.reshape(-1, 16).T, (8, 1)).astype(np.uint16)


def unstriped(offs):
    return offs[:16].T.reshape(-1).astype(np.int64)


K, T, S, N = 512, 2048, 1024, 256


def setup_inputs():
    n = np.random.standard_normal
    s = mx_kscale(K)[:, None]
    return {
        "xT": (n((K, S)) * s).astype(np.float32),
        "w": (n((K, N)) / np.sqrt(K) / s).astype(np.float32),
        "b": (0.3 * n((N, 1))).astype(np.float32),
        "gate": np.tile(np.random.uniform(0.2, 1.0, S), (N, 1)).astype(np.float32),
        "offs": striped(np.sort(np.random.permutation(T)[:S])),
    }


def reference(xT, w, b, gate, offs):
    idx = unstriped(offs)
    xq = mxq(f64(xT), 0, "e4m3")
    y = mxq(f64(w), 0, "e4m3").T @ xq
    y = y + f64(b)
    out = np.zeros((N, T))
    out[:, idx] = f64(gate) * y
    return out

@@ -1,0 +1,161 @@
+from contextlib import ExitStack
+
+import concourse.mybir as mybir
+
+K, T, S, N = 512, 2048, 1024, 256
+FLOPS = 2 * K * N * S
+BYTES = 4 * (K * S + K * N + N + S + N * T) + 2 * 128 * (S // 16)
+
+F32 = mybir.dt.float32
+BF16 = mybir.dt.bfloat16
+U32 = mybir.dt.uint32
+U16 = mybir.dt.uint16
+U8 = mybir.dt.uint8
+FP8X4 = mybir.dt.float8_e4m3fn_x4
+
+P = 128
+PACK = 4
+PIECE = 256
+PIECES = S // PIECE
+M_TILES = N // P
+LIST_COLS = PIECE // 16
+
+
+def interleave(copy, grouped, raw, first, last):
+    if first == last:
+        return
+    copy(
+        out=grouped[:, PACK * first : PACK * last].rearrange("p (c i j) -> p c j i", i=4, j=PACK),
+        in_=raw[:, :, first:last].rearrange("p j (c i) -> p c j i", i=4),
+    )
+
+
+def tile_picked_place_lin_bias_srt_l_kernel(tc, xT, w, b, gate, offs, out):
+    nc = tc.nc
+    mult = mybir.AluOpType.mult
+    identity = mybir.ActivationFunctionType.Identity
+
+    with ExitStack() as ctx:
+        keep = ctx.enter_context(tc.tile_pool(name="keep", bufs=1))
+        psum = ctx.enter_context(tc.psum_pool(name="psum", bufs=1))
+
+        offsets = keep.tile([P, S // 16], U16, name="offsets")
+        bias = keep.tile([P, M_TILES], F32, name="bias")
+        weight_gate = keep.tile([P, S], F32, name="weight_gate")
+        w_raw = keep.tile([P, PACK, N], F32, name="w_raw")
+        x_raw = [keep.tile([P, PACK, PIECE], F32, name=f"x_raw{c}") for c in range(PIECES)]
+        warm = keep.tile([P, 1], F32, name="warm")
+        warmed = keep.tile([P, 1], F32, name="warmed")
+        nc.gpsimd.memset(warm[:], 0.0)
+        nc.scalar.activation(out=warmed[:], in_=warm[:], func=identity)
+
+        xv = xT.rearrange("(p j) s -> p j s", j=PACK)
+
+        def load_x(c):
+            nc.sync.dma_start(out=x_raw[c][:], in_=xv[:, :, PIECE * c : PIECE * (c + 1)])
+
+        def load_gate(first, last):
+            cols = slice(PIECE * first, PIECE * last)
+            nc.sync.dma_start(out=weight_gate[:, cols], in_=gate[0:P, cols])
+
+        def load_w():
+            nc.sync.dma_start(out=w_raw[:], in_=w.rearrange("(p j) m -> p j m", j=PACK))
+
+        def load_bias(eng):
+            eng.dma_start(out=bias[:], in_=b.rearrange("(h p) o -> p (h o)", p=P))
+
+        def load_offs():
+            nc.sync.dma_start(offsets[:], offs)
+
+        load_x(0)
+        load_w()
+        load_x(1)
+        load_bias(nc.sync)
+        load_offs()
+        load_gate(0, 2)
+        load_x(2)
+        load_x(3)
+        load_gate(2, 4)
+
+        windows = [keep.tile([P, T], F32, name=f"window{h}") for h in range(M_TILES)]
+        nc.vector.memset(windows[0][:], 0.0)
+        nc.vector.memset(windows[1][:], 0.0)
+
+        w_grouped = keep.tile([P, PACK * N], BF16, name="w_grouped", align_bytes=64)
+        w_codes = keep.tile([P, N], U32, name="w_codes", align_bytes=64)
+        w_scales = keep.tile([P, N], U8, name="w_scales", align_bytes=64)
+        x_grouped = [keep.tile([P, PACK * PIECE], BF16, name=f"x_grouped{c}", align_bytes=64) for c in range(PIECES)]
+        x_codes = [keep.tile([P, PIECE], U32, name=f"x_codes{c}", align_bytes=64) for c in range(PIECES)]
+        x_scales = [keep.tile([P, PIECE], U8, name=f"x_scales{c}", align_bytes=64) for c in range(PIECES)]
+        y = [keep.tile([P, S], F32, name=f"y{h}") for h in range(M_TILES)]
+        sums = {}
+        for h, segments in enumerate((((0, 1), (1, 2), (2, 3), (3, 4)), ((0, 1), (1, 2), (2, 4)))):
+            for first, last in segments:
+                bank = psum.tile([P, PIECE * (last - first)], F32, name=f"sums{h}_{first}")
+                for c in range(first, last):
+                    sums[c, h] = (bank, first, last)
+
+        vector_cols = (0, 160, 64, 0)
+        w_vector_cols = 128
+
+        def group_x(c):
+            v = vector_cols[c]
+            interleave(nc.scalar.copy, x_grouped[c], x_raw[c], v, PIECE)
+            interleave(nc.vector.tensor_copy, x_grouped[c], x_raw[c], 0, v)
+
+        def quantize_x(c):
+            nc.vector.quantize_mx(out=x_codes[c][:].bitcast(FP8X4), scales=x_scales[c][:], in_=x_grouped[c][:])
+            for h in range(M_TILES):
+                cols = slice(P * h, P * (h + 1))
+                bank, first, last = sums[c, h]
+                nc.tensor.matmul_mx(
+                    out=bank[:, PIECE * (c - first) : PIECE * (c - first + 1)],
+                    lhsT=w_codes[:, cols].bitcast(FP8X4),
+                    lhsT_scale=w_scales[:, cols],
+                    rhs=x_codes[c][:].bitcast(FP8X4),
+                    rhs_scale=x_scales[c][:],
+                    start=True,
+                    stop=True,
+                )
+
+        def add_bias(h, first, last):
+            bank = sums[first, h][0]
+            nc.scalar.activation(out=y[h][:, PIECE * first : PIECE * last], in_=bank[:], func=identity, bias=bias[:, h : h + 1])
+
+        def scatter(h, first, last):
+            nc.vector.tensor_tensor(
+                windows[h][:].indirect(offsets[:, LIST_COLS * first : LIST_COLS * last]),
+                y[h][:, PIECE * first : PIECE * last],
+                weight_gate[:, PIECE * first : PIECE * last],
+                mult,
+            )
+
+        def store(h):
+            nc.sync.dma_start(out=out[P * h : P * (h + 1), :], in_=windows[h][:])
+
+        interleave(nc.vector.tensor_copy, w_grouped, w_raw, 0, w_vector_cols)
+        interleave(nc.scalar.copy, w_grouped, w_raw, w_vector_cols, N)
+        nc.vector.quantize_mx(out=w_codes[:].bitcast(FP8X4), scales=w_scales[:], in_=w_grouped[:])
+        group_x(0)
+        quantize_x(0)
+        add_bias(0, 0, 1)
+        group_x(1)
+        quantize_x(1)
+        scatter(0, 0, 1)
+        add_bias(0, 1, 2)
+        group_x(2)
+        quantize_x(2)
+        scatter(0, 1, 2)
+        add_bias(0, 2, 3)
+        group_x(3)
+        scatter(0, 2, 3)
+        quantize_x(3)
+        add_bias(0, 3, 4)
+        scatter(0, 3, 4)
+        store(0)
+        add_bias(1, 0, 1)
+        add_bias(1, 1, 2)
+        add_bias(1, 2, 4)
+        scatter(1, 0, 1)
+        scatter(1, 1, 4)
+        store(1)

@@ -18,7 +18,9 @@ PACK = 4
 PIECE = 256
 PIECES = S // PIECE
 M_TILES = N // P
-LIST_COLS = PIECE // 16
+BANK = 512
+QUAD = 32
+LEAD = PIECE - 8
 
 
 def interleave(copy, grouped, raw, first, last):
@@ -33,7 +35,7 @@ def interleave(copy, grouped, raw, first, last):
 def tile_picked_place_lin_bias_srt_l_kernel(tc, xT, w, b, gate, offs, out):
     nc = tc.nc
     mult = mybir.AluOpType.mult
-    identity = mybir.ActivationFunctionType.Identity
+    ident_fn = mybir.ActivationFunctionType.Identity
 
     with ExitStack() as ctx:
         keep = ctx.enter_context(tc.tile_pool(name="keep", bufs=1))
@@ -41,121 +43,173 @@ def tile_picked_place_lin_bias_srt_l_kernel(tc, xT, w, b, gate, offs, out):
 
         offsets = keep.tile([P, S // 16], U16, name="offsets")
         bias = keep.tile([P, M_TILES], F32, name="bias")
-        weight_gate = keep.tile([P, S], F32, name="weight_gate")
+        gate_cols = keep.tile([P, S // BANK, 4], F32, name="gate_cols")
+        gate_rows = keep.tile([P, S], F32, name="gate_rows")
         w_raw = keep.tile([P, PACK, N], F32, name="w_raw")
-        x_raw = [keep.tile([P, PACK, PIECE], F32, name=f"x_raw{c}") for c in range(PIECES)]
-        warm = keep.tile([P, 1], F32, name="warm")
+        stage = [keep.tile([P, LEAD + PACK * PIECE + LEAD], F32, name=f"stage{c}") for c in range(PIECES)]
+        x_raw = [stage[c][:, LEAD : LEAD + PACK * PIECE].rearrange("p (j s) -> p j s", j=PACK) for c in range(PIECES)]
+        identity = keep.tile([P, P], F32, name="identity")
+        ones = keep.tile([P, QUAD], F32, name="ones")
+        column = keep.tile([P, QUAD], F32, name="column", align_bytes=64)
+        row = keep.tile([P, QUAD], F32, name="row", align_bytes=64)
+        windows = [keep.tile([P, T], F32, name=f"window{h}") for h in range(M_TILES)]
+        nc.vector.memset(ones[:], 1.0)
+        nc.vector.memset(identity[:], 0.0)
+        nc.vector.tensor_tensor_scan(column[:], ones[:], ones[:], 0.0, mult, mybir.AluOpType.add)
+        nc.vector.transpose(row[:], column[:])
+        for q in range(0, P, QUAD):
+            part = slice(q, q + QUAD)
+            nc.vector.tensor_tensor(identity[part, part], column[part, :], row[part, :], mybir.AluOpType.is_equal)
         warmed = keep.tile([P, 1], F32, name="warmed")
-        nc.gpsimd.memset(warm[:], 0.0)
-        nc.scalar.activation(out=warmed[:], in_=warm[:], func=identity)
 
         xv = xT.rearrange("(p j) s -> p j s", j=PACK)
 
         def load_x(c):
-            nc.sync.dma_start(out=x_raw[c][:], in_=xv[:, :, PIECE * c : PIECE * (c + 1)])
+            nc.sync.dma_start(out=x_raw[c], in_=xv[:, :, PIECE * c : PIECE * (c + 1)])
 
-        def load_gate(first, last):
-            cols = slice(PIECE * first, PIECE * last)
-            nc.sync.dma_start(out=weight_gate[:, cols], in_=gate[0:P, cols])
-
-        def load_w():
-            nc.sync.dma_start(out=w_raw[:], in_=w.rearrange("(p j) m -> p j m", j=PACK))
-
-        def load_bias(eng):
-            eng.dma_start(out=bias[:], in_=b.rearrange("(h p) o -> p (h o)", p=P))
-
-        def load_offs():
-            nc.sync.dma_start(offsets[:], offs)
-
+        nc.sync.dma_start(out=gate_cols[:], in_=gate[0:1, :].rearrange("o (g p c) -> (o p) g c", p=P, c=4))
+        nc.scalar.activation(out=warmed[:], in_=ones[:, 0:1], func=ident_fn)
         load_x(0)
-        load_w()
+        nc.sync.dma_start(out=w_raw[:], in_=w.rearrange("(p j) m -> p j m", j=PACK))
+        nc.sync.dma_start(out=bias[:], in_=b.rearrange("(h p) o -> p (h o)", p=P))
         load_x(1)
-        load_bias(nc.sync)
-        load_offs()
-        load_gate(0, 2)
+        nc.sync.dma_start(offsets[:], offs)
         load_x(2)
         load_x(3)
-        load_gate(2, 4)
 
-        windows = [keep.tile([P, T], F32, name=f"window{h}") for h in range(M_TILES)]
-        nc.vector.memset(windows[0][:], 0.0)
-        nc.vector.memset(windows[1][:], 0.0)
+        for h in range(M_TILES):
+            for half in range(2):
+                nc.vector.memset(windows[h][:, half * T // 2 : (half + 1) * T // 2], 0.0)
 
         w_grouped = keep.tile([P, PACK * N], BF16, name="w_grouped", align_bytes=64)
-        w_codes = keep.tile([P, N], U32, name="w_codes", align_bytes=64)
-        w_scales = keep.tile([P, N], U8, name="w_scales", align_bytes=64)
+        w_codes = [keep.tile([P, P], U32, name=f"w_codes{h}", align_bytes=64) for h in range(M_TILES)]
+        w_scales = [keep.tile([P, P], U8, name=f"w_scales{h}", align_bytes=64) for h in range(M_TILES)]
         x_grouped = [keep.tile([P, PACK * PIECE], BF16, name=f"x_grouped{c}", align_bytes=64) for c in range(PIECES)]
         x_codes = [keep.tile([P, PIECE], U32, name=f"x_codes{c}", align_bytes=64) for c in range(PIECES)]
         x_scales = [keep.tile([P, PIECE], U8, name=f"x_scales{c}", align_bytes=64) for c in range(PIECES)]
-        y = [keep.tile([P, S], F32, name=f"y{h}") for h in range(M_TILES)]
+        y_first = stage[1][:, 2 * LEAD + (PACK - 1) * PIECE :]
+        y0 = [stage[(c + 1) % PIECES][:, :PIECE] for c in range(PIECES)]
+
+        def y(h, first, last):
+            if h == 0:
+                c = first // PIECE
+                return y0[c][:, first - PIECE * c : last - PIECE * c]
+            if first < PIECE:
+                return y_first[:, first:last]
+            return stage[3][:, LEAD + first : LEAD + last]
+
         sums = {}
-        for h, segments in enumerate((((0, 1), (1, 2), (2, 3), (3, 4)), ((0, 1), (1, 2), (2, 4)))):
-            for first, last in segments:
-                bank = psum.tile([P, PIECE * (last - first)], F32, name=f"sums{h}_{first}")
-                for c in range(first, last):
-                    sums[c, h] = (bank, first, last)
 
-        vector_cols = (0, 160, 64, 0)
-        w_vector_cols = 128
+        def spread_gate(g, copy):
+            bank = psum.tile([P, BANK], F32, name=f"gate_bank{g}", tag=f"bank{g}")
+            for c in range(4):
+                nc.tensor.transpose(bank[:, P * c : P * (c + 1)], gate_cols[:, g, c : c + 1].to_broadcast([P, P]), identity[:])
+            copy(
+                out=gate_rows[:, BANK * g : BANK * (g + 1)].rearrange("q (p c) -> q p c", c=4),
+                in_=bank[:].rearrange("q (c p) -> q p c", c=4),
+            )
 
-        def group_x(c):
-            v = vector_cols[c]
-            interleave(nc.scalar.copy, x_grouped[c], x_raw[c], v, PIECE)
-            interleave(nc.vector.tensor_copy, x_grouped[c], x_raw[c], 0, v)
+        def open_bank(tag, *users):
+            bank = psum.tile([P, BANK], F32, name=f"sums_{tag}", tag=tag)
+            for place, user in enumerate(users):
+                sums[user] = (bank, PIECE * place)
+
+        def group_x(c, copy):
+            interleave(copy, x_grouped[c], x_raw[c], 0, PIECE // 2)
+            interleave(copy, x_grouped[c], x_raw[c], PIECE // 2, PIECE)
+
+        def quantize_w(h):
+            nc.vector.quantize_mx(out=w_codes[h][:].bitcast(FP8X4), scales=w_scales[h][:], in_=w_grouped[:, PACK * P * h : PACK * P * (h + 1)])
 
         def quantize_x(c):
             nc.vector.quantize_mx(out=x_codes[c][:].bitcast(FP8X4), scales=x_scales[c][:], in_=x_grouped[c][:])
-            for h in range(M_TILES):
-                cols = slice(P * h, P * (h + 1))
-                bank, first, last = sums[c, h]
-                nc.tensor.matmul_mx(
-                    out=bank[:, PIECE * (c - first) : PIECE * (c - first + 1)],
-                    lhsT=w_codes[:, cols].bitcast(FP8X4),
-                    lhsT_scale=w_scales[:, cols],
-                    rhs=x_codes[c][:].bitcast(FP8X4),
-                    rhs_scale=x_scales[c][:],
-                    start=True,
-                    stop=True,
-                )
+
+        def multiply(h, c):
+            bank, col = sums[h, c]
+            nc.tensor.matmul_mx(
+                out=bank[:, col : col + PIECE],
+                lhsT=w_codes[h][:].bitcast(FP8X4),
+                lhsT_scale=w_scales[h][:],
+                rhs=x_codes[c][:].bitcast(FP8X4),
+                rhs_scale=x_scales[c][:],
+                start=True,
+                stop=True,
+            )
+
+        done = [keep.tile([P, 2 * PIECE], F32, name="done0"), keep.tile([P, PIECE], F32, name="done1")]
+        bias_copies = {(0, 1): x_grouped[3][:, 0:2].bitcast(F32), (0, 3): done[0][:, 0:1], (1, 3): done[1][:, 0:1]}
 
         def add_bias(h, first, last):
-            bank = sums[first, h][0]
-            nc.scalar.activation(out=y[h][:, PIECE * first : PIECE * last], in_=bank[:], func=identity, bias=bias[:, h : h + 1])
+            column_of_bias = bias_copies.get((h, first), bias[:, h : h + 1])
+            bank, col = sums[h, first]
+            nc.scalar.activation(
+                out=y(h, PIECE * first, PIECE * last), in_=bank[:, col : col + PIECE * (last - first)], func=ident_fn, bias=column_of_bias
+            )
 
         def scatter(h, first, last):
             nc.vector.tensor_tensor(
-                windows[h][:].indirect(offsets[:, LIST_COLS * first : LIST_COLS * last]),
-                y[h][:, PIECE * first : PIECE * last],
-                weight_gate[:, PIECE * first : PIECE * last],
+                windows[h][:].indirect(offsets[:, first // 16 : last // 16]),
+                y(h, first, last),
+                gate_rows[:, first:last],
                 mult,
             )
 
-        def store(h):
-            nc.sync.dma_start(out=out[P * h : P * (h + 1), :], in_=windows[h][:])
+        def store_through(h, first, last):
+            nc.scalar.copy(out=done[h][:], in_=windows[h][:, first:last])
+            nc.sync.dma_start(out=out[P * h : P * (h + 1), first:last], in_=done[h][:])
 
-        interleave(nc.vector.tensor_copy, w_grouped, w_raw, 0, w_vector_cols)
-        interleave(nc.scalar.copy, w_grouped, w_raw, w_vector_cols, N)
-        nc.vector.quantize_mx(out=w_codes[:].bitcast(FP8X4), scales=w_scales[:], in_=w_grouped[:])
-        group_x(0)
+        def store(h, first, last):
+            nc.sync.dma_start(out=out[P * h : P * (h + 1), first:last], in_=windows[h][:, first:last])
+
+        spread_gate(0, nc.scalar.copy)
+        spread_gate(1, nc.scalar.copy)
+        open_bank("bank2", (0, 0))
+        open_bank("bank3", (1, 0))
+        open_bank("bank4", (0, 1), (1, 1))
+        open_bank("bank5", (0, 2), (1, 2))
+        open_bank("bank6", (0, 3))
+        open_bank("bank7", (1, 3))
+        interleave(nc.vector.tensor_copy, x_grouped[0], x_raw[0], 0, PIECE)
         quantize_x(0)
-        add_bias(0, 0, 1)
-        group_x(1)
-        quantize_x(1)
-        scatter(0, 0, 1)
-        add_bias(0, 1, 2)
-        group_x(2)
-        quantize_x(2)
-        scatter(0, 1, 2)
-        add_bias(0, 2, 3)
-        group_x(3)
-        scatter(0, 2, 3)
-        quantize_x(3)
-        add_bias(0, 3, 4)
-        scatter(0, 3, 4)
-        store(0)
+        interleave(nc.vector.tensor_copy, w_grouped, w_raw, 0, P)
+        interleave(nc.scalar.copy, w_grouped, w_raw, P, N)
+        for (h, c), place in bias_copies.items():
+            nc.scalar.copy(out=place, in_=bias[:, h : h + 1])
+        quantize_w(0)
+        multiply(0, 0)
+        quantize_w(1)
+        multiply(1, 0)
+        interleave(nc.vector.tensor_copy, x_grouped[1], x_raw[1], PIECE // 2, PIECE)
+        interleave(nc.vector.tensor_copy, x_grouped[1], x_raw[1], 0, PIECE // 2)
         add_bias(1, 0, 1)
+        add_bias(0, 0, 1)
+        quantize_x(1)
+        multiply(0, 1)
+        scatter(1, 0, 256)
+        scatter(0, 0, 256)
+        store(1, 0, 256)
+        interleave(nc.scalar.copy, x_grouped[2], x_raw[2], 0, PIECE)
+        quantize_x(2)
+        multiply(0, 2)
+        add_bias(0, 1, 2)
+        scatter(0, 256, 512)
+        multiply(1, 1)
+        interleave(nc.vector.tensor_copy, x_grouped[3], x_raw[3], PIECE // 2, PIECE)
+        interleave(nc.scalar.copy, x_grouped[3], x_raw[3], 0, PIECE // 2)
+        quantize_x(3)
+        multiply(0, 3)
+        add_bias(0, 2, 3)
+        scatter(0, 512, 768)
+        multiply(1, 2)
         add_bias(1, 1, 2)
-        add_bias(1, 2, 4)
-        scatter(1, 0, 1)
-        scatter(1, 1, 4)
-        store(1)
+        scatter(1, 256, 512)
+        add_bias(1, 2, 3)
+        add_bias(0, 3, 4)
+        multiply(1, 3)
+        store_through(0, 0, 512)
+        scatter(0, 768, 1024)
+        store(0, 512, T)
+        add_bias(1, 3, 4)
+        store_through(1, 256, 512)
+        scatter(1, 512, 1024)
+        store(1, 512, T)

@@ -43,7 +43,7 @@ def tile_picked_place_lin_bias_srt_l_kernel(tc, xT, w, b, gate, offs, out):
 
         offsets = keep.tile([P, S // 16], U16, name="offsets")
         bias = keep.tile([P, M_TILES], F32, name="bias")
-        gate_cols = keep.tile([P, S // BANK, 4], F32, name="gate_cols")
+        gate_cols = keep.tile([P, S // P], F32, name="gate_cols")
         gate_rows = keep.tile([P, S], F32, name="gate_rows")
         w_raw = keep.tile([P, PACK, N], F32, name="w_raw")
         stage = [keep.tile([P, LEAD + PACK * PIECE + LEAD], F32, name=f"stage{c}") for c in range(PIECES)]
@@ -53,6 +53,8 @@ def tile_picked_place_lin_bias_srt_l_kernel(tc, xT, w, b, gate, offs, out):
         column = keep.tile([P, QUAD], F32, name="column", align_bytes=64)
         row = keep.tile([P, QUAD], F32, name="row", align_bytes=64)
         windows = [keep.tile([P, T], F32, name=f"window{h}") for h in range(M_TILES)]
+        zero = keep.tile([P, 1], F32, name="zero")
+        nc.vector.memset(zero[:], 0.0)
         nc.vector.memset(ones[:], 1.0)
         nc.vector.memset(identity[:], 0.0)
         nc.vector.tensor_tensor_scan(column[:], ones[:], ones[:], 0.0, mult, mybir.AluOpType.add)
@@ -64,14 +66,16 @@ def tile_picked_place_lin_bias_srt_l_kernel(tc, xT, w, b, gate, offs, out):
 
         xv = xT.rearrange("(p j) s -> p j s", j=PACK)
 
+        out_rows = out.rearrange("(p h) t -> h p t", h=M_TILES)
+
         def load_x(c):
             nc.sync.dma_start(out=x_raw[c], in_=xv[:, :, PIECE * c : PIECE * (c + 1)])
 
-        nc.sync.dma_start(out=gate_cols[:], in_=gate[0:1, :].rearrange("o (g p c) -> (o p) g c", p=P, c=4))
+        nc.sync.dma_start(out=gate_cols[:], in_=gate[0:1, :].rearrange("o (p c) -> (o p) c", p=P))
         nc.scalar.activation(out=warmed[:], in_=ones[:, 0:1], func=ident_fn)
         load_x(0)
         nc.sync.dma_start(out=w_raw[:], in_=w.rearrange("(p j) m -> p j m", j=PACK))
-        nc.sync.dma_start(out=bias[:], in_=b.rearrange("(h p) o -> p (h o)", p=P))
+        nc.sync.dma_start(out=bias[:], in_=b.rearrange("(p h) o -> p (h o)", p=P))
         load_x(1)
         nc.sync.dma_start(offsets[:], offs)
         load_x(2)
@@ -79,7 +83,7 @@ def tile_picked_place_lin_bias_srt_l_kernel(tc, xT, w, b, gate, offs, out):
 
         for h in range(M_TILES):
             for half in range(2):
-                nc.vector.memset(windows[h][:, half * T // 2 : (half + 1) * T // 2], 0.0)
+                nc.vector.tensor_copy(out=windows[h][:, half * T // 2 : (half + 1) * T // 2], in_=zero[:].to_broadcast([P, T // 2]))
 
         w_grouped = keep.tile([P, PACK * N], BF16, name="w_grouped", align_bytes=64)
         w_codes = [keep.tile([P, P], U32, name=f"w_codes{h}", align_bytes=64) for h in range(M_TILES)]
@@ -103,9 +107,9 @@ def tile_picked_place_lin_bias_srt_l_kernel(tc, xT, w, b, gate, offs, out):
         def spread_gate(g, copy):
             bank = psum.tile([P, BANK], F32, name=f"gate_bank{g}", tag=f"bank{g}")
             for c in range(4):
-                nc.tensor.transpose(bank[:, P * c : P * (c + 1)], gate_cols[:, g, c : c + 1].to_broadcast([P, P]), identity[:])
+                nc.tensor.transpose(bank[:, P * c : P * (c + 1)], gate_cols[:, 4 * g + c : 4 * g + c + 1].to_broadcast([P, P]), identity[:])
             copy(
-                out=gate_rows[:, BANK * g : BANK * (g + 1)].rearrange("q (p c) -> q p c", c=4),
+                out=gate_rows[:].rearrange("q (p c) -> q p c", c=S // P)[:, :, 4 * g : 4 * g + 4],
                 in_=bank[:].rearrange("q (c p) -> q p c", c=4),
             )
 
@@ -118,11 +122,17 @@ def tile_picked_place_lin_bias_srt_l_kernel(tc, xT, w, b, gate, offs, out):
             interleave(copy, x_grouped[c], x_raw[c], 0, PIECE // 2)
             interleave(copy, x_grouped[c], x_raw[c], PIECE // 2, PIECE)
 
+        def group_w(h, copy):
+            columns = w_raw[:].rearrange("p j (m h) -> p j h m", h=M_TILES)[:, :, h, :]
+            interleave(copy, w_grouped[:, PACK * P * h : PACK * P * (h + 1)], columns, 0, P)
+
         def quantize_w(h):
             nc.vector.quantize_mx(out=w_codes[h][:].bitcast(FP8X4), scales=w_scales[h][:], in_=w_grouped[:, PACK * P * h : PACK * P * (h + 1)])
 
-        def quantize_x(c):
-            nc.vector.quantize_mx(out=x_codes[c][:].bitcast(FP8X4), scales=x_scales[c][:], in_=x_grouped[c][:])
+        def quantize_x(c, first=0, last=PIECE):
+            nc.vector.quantize_mx(
+                out=x_codes[c][:, first:last].bitcast(FP8X4), scales=x_scales[c][:, first:last], in_=x_grouped[c][:, PACK * first : PACK * last]
+            )
 
         def multiply(h, c):
             bank, col = sums[h, c]
@@ -156,23 +166,23 @@ def tile_picked_place_lin_bias_srt_l_kernel(tc, xT, w, b, gate, offs, out):
 
         def store_through(h, first, last):
             nc.scalar.copy(out=done[h][:], in_=windows[h][:, first:last])
-            nc.sync.dma_start(out=out[P * h : P * (h + 1), first:last], in_=done[h][:])
+            nc.sync.dma_start(out=out_rows[h, :, first:last], in_=done[h][:])
 
         def store(h, first, last):
-            nc.sync.dma_start(out=out[P * h : P * (h + 1), first:last], in_=windows[h][:, first:last])
+            nc.sync.dma_start(out=out_rows[h, :, first:last], in_=windows[h][:, first:last])
 
         spread_gate(0, nc.scalar.copy)
         spread_gate(1, nc.scalar.copy)
         open_bank("bank2", (0, 0))
         open_bank("bank3", (1, 0))
         open_bank("bank4", (0, 1), (1, 1))
-        open_bank("bank5", (0, 2), (1, 2))
-        open_bank("bank6", (0, 3))
-        open_bank("bank7", (1, 3))
+        open_bank("bank5", (0, 2))
+        open_bank("bank6", (0, 3), (1, 3))
+        open_bank("bank7", (1, 2))
         interleave(nc.vector.tensor_copy, x_grouped[0], x_raw[0], 0, PIECE)
         quantize_x(0)
-        interleave(nc.vector.tensor_copy, w_grouped, w_raw, 0, P)
-        interleave(nc.scalar.copy, w_grouped, w_raw, P, N)
+        group_w(0, nc.vector.tensor_copy)
+        group_w(1, nc.scalar.copy)
         for (h, c), place in bias_copies.items():
             nc.scalar.copy(out=place, in_=bias[:, h : h + 1])
         quantize_w(0)
@@ -183,7 +193,8 @@ def tile_picked_place_lin_bias_srt_l_kernel(tc, xT, w, b, gate, offs, out):
         interleave(nc.vector.tensor_copy, x_grouped[1], x_raw[1], 0, PIECE // 2)
         add_bias(1, 0, 1)
         add_bias(0, 0, 1)
-        quantize_x(1)
+        quantize_x(1, PIECE // 2, PIECE)
+        quantize_x(1, 0, PIECE // 2)
         multiply(0, 1)
         scatter(1, 0, 256)
         scatter(0, 0, 256)

@@ -19,7 +19,6 @@ PIECE = 256
 PIECES = S // PIECE
 M_TILES = N // P
 BANK = 512
-QUAD = 32
 LEAD = PIECE - 8
 
 
@@ -43,25 +42,13 @@ def tile_picked_place_lin_bias_srt_l_kernel(tc, xT, w, b, gate, offs, out):
 
         offsets = keep.tile([P, S // 16], U16, name="offsets")
         bias = keep.tile([P, M_TILES], F32, name="bias")
-        gate_cols = keep.tile([P, S // P], F32, name="gate_cols")
         gate_rows = keep.tile([P, S], F32, name="gate_rows")
         w_raw = keep.tile([P, PACK, N], F32, name="w_raw")
         stage = [keep.tile([P, LEAD + PACK * PIECE + LEAD], F32, name=f"stage{c}") for c in range(PIECES)]
         x_raw = [stage[c][:, LEAD : LEAD + PACK * PIECE].rearrange("p (j s) -> p j s", j=PACK) for c in range(PIECES)]
-        identity = keep.tile([P, P], F32, name="identity")
-        ones = keep.tile([P, QUAD], F32, name="ones")
-        column = keep.tile([P, QUAD], F32, name="column", align_bytes=64)
-        row = keep.tile([P, QUAD], F32, name="row", align_bytes=64)
         windows = [keep.tile([P, T], F32, name=f"window{h}") for h in range(M_TILES)]
         zero = keep.tile([P, 1], F32, name="zero")
         nc.vector.memset(zero[:], 0.0)
-        nc.vector.memset(ones[:], 1.0)
-        nc.vector.memset(identity[:], 0.0)
-        nc.vector.tensor_tensor_scan(column[:], ones[:], ones[:], 0.0, mult, mybir.AluOpType.add)
-        nc.vector.transpose(row[:], column[:])
-        for q in range(0, P, QUAD):
-            part = slice(q, q + QUAD)
-            nc.vector.tensor_tensor(identity[part, part], column[part, :], row[part, :], mybir.AluOpType.is_equal)
         warmed = keep.tile([P, 1], F32, name="warmed")
 
         xv = xT.rearrange("(p j) s -> p j s", j=PACK)
@@ -71,15 +58,19 @@ def tile_picked_place_lin_bias_srt_l_kernel(tc, xT, w, b, gate, offs, out):
         def load_x(c):
             nc.sync.dma_start(out=x_raw[c], in_=xv[:, :, PIECE * c : PIECE * (c + 1)])
 
-        nc.sync.dma_start(out=gate_cols[:], in_=gate[0:1, :].rearrange("o (p c) -> (o p) c", p=P))
-        nc.scalar.activation(out=warmed[:], in_=ones[:, 0:1], func=ident_fn)
+        def load_gate(g):
+            nc.sync.dma_start(out=gate_rows[:, BANK * g : BANK * (g + 1)], in_=gate[0:P, BANK * g : BANK * (g + 1)])
+
+        nc.scalar.activation(out=warmed[:], in_=zero[:], func=ident_fn)
         load_x(0)
         nc.sync.dma_start(out=w_raw[:], in_=w.rearrange("(p j) m -> p j m", j=PACK))
-        nc.sync.dma_start(out=bias[:], in_=b.rearrange("(p h) o -> p (h o)", p=P))
         load_x(1)
+        nc.sync.dma_start(out=bias[:], in_=b.rearrange("(p h) o -> p (h o)", p=P))
         nc.sync.dma_start(offsets[:], offs)
+        load_gate(0)
         load_x(2)
         load_x(3)
+        load_gate(1)
 
         for h in range(M_TILES):
             for half in range(2):
@@ -103,15 +94,6 @@ def tile_picked_place_lin_bias_srt_l_kernel(tc, xT, w, b, gate, offs, out):
             return stage[3][:, LEAD + first : LEAD + last]
 
         sums = {}
-
-        def spread_gate(g, copy):
-            bank = psum.tile([P, BANK], F32, name=f"gate_bank{g}", tag=f"bank{g}")
-            for c in range(4):
-                nc.tensor.transpose(bank[:, P * c : P * (c + 1)], gate_cols[:, 4 * g + c : 4 * g + c + 1].to_broadcast([P, P]), identity[:])
-            copy(
-                out=gate_rows[:].rearrange("q (p c) -> q p c", c=S // P)[:, :, 4 * g : 4 * g + 4],
-                in_=bank[:].rearrange("q (c p) -> q p c", c=4),
-            )
 
         def open_bank(tag, *users):
             bank = psum.tile([P, BANK], F32, name=f"sums_{tag}", tag=tag)
@@ -171,8 +153,6 @@ def tile_picked_place_lin_bias_srt_l_kernel(tc, xT, w, b, gate, offs, out):
         def store(h, first, last):
             nc.sync.dma_start(out=out_rows[h, :, first:last], in_=windows[h][:, first:last])
 
-        spread_gate(0, nc.scalar.copy)
-        spread_gate(1, nc.scalar.copy)
         open_bank("bank2", (0, 0))
         open_bank("bank3", (1, 0))
         open_bank("bank4", (0, 1), (1, 1))

@@ -16,15 +16,15 @@ FP8X4 = mybir.dt.float8_e4m3fn_x4
 P = 128
 PACK = 4
 PIECE = 256
+HALF = PIECE // 2
 PIECES = S // PIECE
-M_TILES = N // P
+ROW_TILES = N // P
 BANK = 512
-LEAD = PIECE - 8
+SHARED = 8
+MARGIN = PIECE - SHARED
 
 
 def interleave(copy, grouped, raw, first, last):
-    if first == last:
-        return
     copy(
         out=grouped[:, PACK * first : PACK * last].rearrange("p (c i j) -> p c j i", i=4, j=PACK),
         in_=raw[:, :, first:last].rearrange("p j (c i) -> p c j i", i=4),
@@ -33,93 +33,106 @@ def interleave(copy, grouped, raw, first, last):
 
 def tile_picked_place_lin_bias_srt_l_kernel(tc, xT, w, b, gate, offs, out):
     nc = tc.nc
-    mult = mybir.AluOpType.mult
-    ident_fn = mybir.ActivationFunctionType.Identity
+    identity = mybir.ActivationFunctionType.Identity
 
     with ExitStack() as ctx:
         keep = ctx.enter_context(tc.tile_pool(name="keep", bufs=1))
         psum = ctx.enter_context(tc.psum_pool(name="psum", bufs=1))
 
         offsets = keep.tile([P, S // 16], U16, name="offsets")
-        bias = keep.tile([P, M_TILES], F32, name="bias")
+        bias = keep.tile([P, ROW_TILES], F32, name="bias")
         gate_rows = keep.tile([P, S], F32, name="gate_rows")
         w_raw = keep.tile([P, PACK, N], F32, name="w_raw")
-        stage = [keep.tile([P, LEAD + PACK * PIECE + LEAD], F32, name=f"stage{c}") for c in range(PIECES)]
-        x_raw = [stage[c][:, LEAD : LEAD + PACK * PIECE].rearrange("p (j s) -> p j s", j=PACK) for c in range(PIECES)]
-        windows = [keep.tile([P, T], F32, name=f"window{h}") for h in range(M_TILES)]
+        stage = [keep.tile([P, MARGIN + PACK * PIECE + MARGIN], F32, name=f"stage{c}") for c in range(PIECES)]
+        x_raw = [stage[c][:, MARGIN : MARGIN + PACK * PIECE].rearrange("p (j s) -> p j s", j=PACK) for c in range(PIECES)]
+        windows = [keep.tile([P, T], F32, name=f"window{h}") for h in range(ROW_TILES)]
         zero = keep.tile([P, 1], F32, name="zero")
-        nc.vector.memset(zero[:], 0.0)
         warmed = keep.tile([P, 1], F32, name="warmed")
+        nc.vector.memset(zero[:], 0.0)
 
-        xv = xT.rearrange("(p j) s -> p j s", j=PACK)
-
-        out_rows = out.rearrange("(p h) t -> h p t", h=M_TILES)
+        x_rows = xT.rearrange("(p j) s -> p j s", j=PACK)
+        out_rows = out.rearrange("(p h) t -> h p t", h=ROW_TILES)
 
         def load_x(c):
-            nc.sync.dma_start(out=x_raw[c], in_=xv[:, :, PIECE * c : PIECE * (c + 1)])
+            nc.sync.dma_start(out=x_raw[c], in_=x_rows[:, :, PIECE * c : PIECE * (c + 1)])
 
-        def load_gate(g):
-            nc.sync.dma_start(out=gate_rows[:, BANK * g : BANK * (g + 1)], in_=gate[0:P, BANK * g : BANK * (g + 1)])
+        def load_gate(first, last):
+            nc.sync.dma_start(out=gate_rows[:, first:last], in_=gate[0:P, first:last])
 
-        nc.scalar.activation(out=warmed[:], in_=zero[:], func=ident_fn)
+        nc.scalar.dma_start(out=bias[:], in_=b.rearrange("(p h) o -> p (h o)", p=P))
+        nc.scalar.activation(out=warmed[:], in_=zero[:], func=identity)
         load_x(0)
         nc.sync.dma_start(out=w_raw[:], in_=w.rearrange("(p j) m -> p j m", j=PACK))
         load_x(1)
-        nc.sync.dma_start(out=bias[:], in_=b.rearrange("(p h) o -> p (h o)", p=P))
         nc.sync.dma_start(offsets[:], offs)
-        load_gate(0)
+        load_gate(0, S // 2)
         load_x(2)
         load_x(3)
-        load_gate(1)
+        load_gate(S // 2, S)
 
-        for h in range(M_TILES):
-            for half in range(2):
-                nc.vector.tensor_copy(out=windows[h][:, half * T // 2 : (half + 1) * T // 2], in_=zero[:].to_broadcast([P, T // 2]))
+        for h in range(ROW_TILES):
+            for first in (0, T // 2):
+                nc.vector.tensor_copy(out=windows[h][:, first : first + T // 2], in_=zero[:].to_broadcast([P, T // 2]))
 
         w_grouped = keep.tile([P, PACK * N], BF16, name="w_grouped", align_bytes=64)
-        w_codes = [keep.tile([P, P], U32, name=f"w_codes{h}", align_bytes=64) for h in range(M_TILES)]
-        w_scales = [keep.tile([P, P], U8, name=f"w_scales{h}", align_bytes=64) for h in range(M_TILES)]
+        w_codes = [keep.tile([P, P], U32, name=f"w_codes{h}", align_bytes=64) for h in range(ROW_TILES)]
+        w_scales = [keep.tile([P, P], U8, name=f"w_scales{h}", align_bytes=64) for h in range(ROW_TILES)]
         x_grouped = [keep.tile([P, PACK * PIECE], BF16, name=f"x_grouped{c}", align_bytes=64) for c in range(PIECES)]
         x_codes = [keep.tile([P, PIECE], U32, name=f"x_codes{c}", align_bytes=64) for c in range(PIECES)]
         x_scales = [keep.tile([P, PIECE], U8, name=f"x_scales{c}", align_bytes=64) for c in range(PIECES)]
-        y_first = stage[1][:, 2 * LEAD + (PACK - 1) * PIECE :]
-        y0 = [stage[(c + 1) % PIECES][:, :PIECE] for c in range(PIECES)]
 
-        def y(h, first, last):
+        sums_front = [stage[(c + 1) % PIECES][:, :PIECE] for c in range(PIECES)]
+        sums_back = stage[1][:, 2 * MARGIN + (PACK - 1) * PIECE :]
+        sums_late = keep.tile([P, S - PIECE], F32, name="sums_late")
+
+        def sums(h, first, last):
             if h == 0:
                 c = first // PIECE
-                return y0[c][:, first - PIECE * c : last - PIECE * c]
+                return sums_front[c][:, first - PIECE * c : last - PIECE * c]
             if first < PIECE:
-                return y_first[:, first:last]
-            return stage[3][:, LEAD + first : LEAD + last]
+                return sums_back[:, first:last]
+            return sums_late[:, first - PIECE : last - PIECE]
 
-        sums = {}
+        final = [keep.tile([P, 2 * PIECE], F32, name="final0"), keep.tile([P, PIECE], F32, name="final1")]
 
-        def open_bank(tag, *users):
-            bank = psum.tile([P, BANK], F32, name=f"sums_{tag}", tag=tag)
-            for place, user in enumerate(users):
-                sums[user] = (bank, PIECE * place)
+        bias_copies = {
+            PIECE: x_grouped[3][:, 0:2].bitcast(F32),
+            2 * PIECE: sums_late[:, 0:1],
+            3 * PIECE: final[0][:, 0:1],
+            3 * PIECE + HALF: final[1][:, 0:1],
+        }
 
-        def group_x(c, copy):
-            interleave(copy, x_grouped[c], x_raw[c], 0, PIECE // 2)
-            interleave(copy, x_grouped[c], x_raw[c], PIECE // 2, PIECE)
+        products = {}
+        for tenants in (((0, 0),), ((1, 0),), ((0, 1),), ((0, 2),), ((1, 1), (1, 2)), ((0, 3), (1, 3))):
+            bank = psum.tile([P, BANK], F32, name="bank%d_%d" % tenants[0])
+            for place, tenant in enumerate(tenants):
+                products[tenant] = (bank, PIECE * place)
 
-        def group_w(h, copy):
-            columns = w_raw[:].rearrange("p j (m h) -> p j h m", h=M_TILES)[:, :, h, :]
+        def group_x(copy, c, first, last):
+            interleave(copy, x_grouped[c], x_raw[c], first, last)
+
+        def group_w(copy, h):
+            columns = w_raw[:].rearrange("p j (i h) -> p j h i", h=ROW_TILES)[:, :, h, :]
             interleave(copy, w_grouped[:, PACK * P * h : PACK * P * (h + 1)], columns, 0, P)
 
         def quantize_w(h):
-            nc.vector.quantize_mx(out=w_codes[h][:].bitcast(FP8X4), scales=w_scales[h][:], in_=w_grouped[:, PACK * P * h : PACK * P * (h + 1)])
-
-        def quantize_x(c, first=0, last=PIECE):
             nc.vector.quantize_mx(
-                out=x_codes[c][:, first:last].bitcast(FP8X4), scales=x_scales[c][:, first:last], in_=x_grouped[c][:, PACK * first : PACK * last]
+                out=w_codes[h][:].bitcast(FP8X4),
+                scales=w_scales[h][:],
+                in_=w_grouped[:, PACK * P * h : PACK * P * (h + 1)],
+            )
+
+        def quantize_x(c, first, last):
+            nc.vector.quantize_mx(
+                out=x_codes[c][:, first:last].bitcast(FP8X4),
+                scales=x_scales[c][:, first:last],
+                in_=x_grouped[c][:, PACK * first : PACK * last],
             )
 
         def multiply(h, c):
-            bank, col = sums[h, c]
+            bank, column = products[h, c]
             nc.tensor.matmul_mx(
-                out=bank[:, col : col + PIECE],
+                out=bank[:, column : column + PIECE],
                 lhsT=w_codes[h][:].bitcast(FP8X4),
                 lhsT_scale=w_scales[h][:],
                 rhs=x_codes[c][:].bitcast(FP8X4),
@@ -128,79 +141,76 @@ def tile_picked_place_lin_bias_srt_l_kernel(tc, xT, w, b, gate, offs, out):
                 stop=True,
             )
 
-        done = [keep.tile([P, 2 * PIECE], F32, name="done0"), keep.tile([P, PIECE], F32, name="done1")]
-        bias_copies = {(0, 1): x_grouped[3][:, 0:2].bitcast(F32), (0, 3): done[0][:, 0:1], (1, 3): done[1][:, 0:1]}
-
         def add_bias(h, first, last):
-            column_of_bias = bias_copies.get((h, first), bias[:, h : h + 1])
-            bank, col = sums[h, first]
+            bank, column = products[h, first // PIECE]
+            column = column + first % PIECE
             nc.scalar.activation(
-                out=y(h, PIECE * first, PIECE * last), in_=bank[:, col : col + PIECE * (last - first)], func=ident_fn, bias=column_of_bias
+                out=sums(h, first, last),
+                in_=bank[:, column : column + last - first],
+                func=identity,
+                bias=bias_copies[first] if h == 0 and first in bias_copies else bias[:, h : h + 1],
             )
 
         def scatter(h, first, last):
             nc.vector.tensor_tensor(
                 windows[h][:].indirect(offsets[:, first // 16 : last // 16]),
-                y(h, first, last),
+                sums(h, first, last),
                 gate_rows[:, first:last],
-                mult,
+                mybir.AluOpType.mult,
             )
-
-        def store_through(h, first, last):
-            nc.scalar.copy(out=done[h][:], in_=windows[h][:, first:last])
-            nc.sync.dma_start(out=out_rows[h, :, first:last], in_=done[h][:])
 
         def store(h, first, last):
             nc.sync.dma_start(out=out_rows[h, :, first:last], in_=windows[h][:, first:last])
 
-        open_bank("bank2", (0, 0))
-        open_bank("bank3", (1, 0))
-        open_bank("bank4", (0, 1), (1, 1))
-        open_bank("bank5", (0, 2))
-        open_bank("bank6", (0, 3), (1, 3))
-        open_bank("bank7", (1, 2))
-        interleave(nc.vector.tensor_copy, x_grouped[0], x_raw[0], 0, PIECE)
-        quantize_x(0)
-        group_w(0, nc.vector.tensor_copy)
-        group_w(1, nc.scalar.copy)
-        for (h, c), place in bias_copies.items():
-            nc.scalar.copy(out=place, in_=bias[:, h : h + 1])
-        quantize_w(0)
-        multiply(0, 0)
-        quantize_w(1)
-        multiply(1, 0)
-        interleave(nc.vector.tensor_copy, x_grouped[1], x_raw[1], PIECE // 2, PIECE)
-        interleave(nc.vector.tensor_copy, x_grouped[1], x_raw[1], 0, PIECE // 2)
-        add_bias(1, 0, 1)
-        add_bias(0, 0, 1)
-        quantize_x(1, PIECE // 2, PIECE)
-        quantize_x(1, 0, PIECE // 2)
+        def store_final(queue, h, first, last):
+            nc.scalar.copy(out=final[h][:], in_=windows[h][:, first:last])
+            queue.dma_start(out=out_rows[h, :, first:last], in_=final[h][:])
+
+        group_x(nc.vector.tensor_copy, 0, 0, PIECE)
+        quantize_x(0, 0, PIECE)
+        group_w(nc.vector.tensor_copy, 0)
+        group_w(nc.scalar.copy, 1)
+        for place in bias_copies.values():
+            nc.scalar.copy(out=place, in_=bias[:, 0:1])
+        for h in range(ROW_TILES):
+            quantize_w(h)
+            multiply(h, 0)
+
+        group_x(nc.vector.tensor_copy, 1, HALF, PIECE)
+        group_x(nc.vector.tensor_copy, 1, 0, HALF)
+        add_bias(1, 0, PIECE)
+        add_bias(0, 0, PIECE)
+        quantize_x(1, HALF, PIECE)
+        quantize_x(1, 0, HALF)
         multiply(0, 1)
-        scatter(1, 0, 256)
-        scatter(0, 0, 256)
-        store(1, 0, 256)
-        interleave(nc.scalar.copy, x_grouped[2], x_raw[2], 0, PIECE)
-        quantize_x(2)
+        scatter(1, 0, PIECE)
+        scatter(0, 0, PIECE)
+        store(1, 0, PIECE)
+
+        group_x(nc.scalar.copy, 2, 0, PIECE)
+        quantize_x(2, 0, PIECE)
         multiply(0, 2)
-        add_bias(0, 1, 2)
-        scatter(0, 256, 512)
+        add_bias(0, PIECE, 2 * PIECE)
+        scatter(0, PIECE, 2 * PIECE)
         multiply(1, 1)
-        interleave(nc.vector.tensor_copy, x_grouped[3], x_raw[3], PIECE // 2, PIECE)
-        interleave(nc.scalar.copy, x_grouped[3], x_raw[3], 0, PIECE // 2)
-        quantize_x(3)
-        multiply(0, 3)
-        add_bias(0, 2, 3)
-        scatter(0, 512, 768)
         multiply(1, 2)
-        add_bias(1, 1, 2)
-        scatter(1, 256, 512)
-        add_bias(1, 2, 3)
-        add_bias(0, 3, 4)
+
+        group_x(nc.vector.tensor_copy, 3, HALF, PIECE)
+        group_x(nc.scalar.copy, 3, 0, HALF)
+        quantize_x(3, 0, PIECE)
+        multiply(0, 3)
+        add_bias(0, 2 * PIECE, 3 * PIECE)
+        scatter(0, 2 * PIECE, 3 * PIECE)
+
+        add_bias(1, PIECE, 3 * PIECE)
+        scatter(1, PIECE, 2 * PIECE)
+        add_bias(0, 3 * PIECE, 3 * PIECE + HALF)
+        add_bias(0, 3 * PIECE + HALF, S)
         multiply(1, 3)
-        store_through(0, 0, 512)
-        scatter(0, 768, 1024)
-        store(0, 512, T)
-        add_bias(1, 3, 4)
-        store_through(1, 256, 512)
-        scatter(1, 512, 1024)
-        store(1, 512, T)
+        store_final(nc.sync, 0, 0, 2 * PIECE)
+        scatter(0, 3 * PIECE, S)
+        store(0, 2 * PIECE, T)
+        store_final(nc.scalar, 1, PIECE, 2 * PIECE)
+        add_bias(1, 3 * PIECE, S)
+        scatter(1, 2 * PIECE, S)
+        store(1, 2 * PIECE, T)

@@ -65,10 +65,11 @@ def tile_picked_place_lin_bias_srt_l_kernel(tc, xT, w, b, gate, offs, out):
         nc.sync.dma_start(out=w_raw[:], in_=w.rearrange("(p j) m -> p j m", j=PACK))
         load_x(1)
         nc.sync.dma_start(offsets[:], offs)
-        load_gate(0, S // 2)
+        load_gate(0, PIECE)
         load_x(2)
+        load_gate(PIECE, 2 * PIECE)
         load_x(3)
-        load_gate(S // 2, S)
+        load_gate(2 * PIECE, S)
 
         for h in range(ROW_TILES):
             for first in (0, T // 2):
@@ -103,7 +104,7 @@ def tile_picked_place_lin_bias_srt_l_kernel(tc, xT, w, b, gate, offs, out):
         }
 
         products = {}
-        for tenants in (((0, 0),), ((1, 0),), ((0, 1),), ((0, 2),), ((1, 1), (1, 2)), ((0, 3), (1, 3))):
+        for tenants in (((0, 0),), ((1, 0),), ((0, 1),), ((0, 2),), ((1, 1), (1, 2)), ((0, 3),), ((1, 3),)):
             bank = psum.tile([P, BANK], F32, name="bank%d_%d" % tenants[0])
             for place, tenant in enumerate(tenants):
                 products[tenant] = (bank, PIECE * place)
@@ -207,10 +208,10 @@ def tile_picked_place_lin_bias_srt_l_kernel(tc, xT, w, b, gate, offs, out):
         add_bias(0, 3 * PIECE, 3 * PIECE + HALF)
         add_bias(0, 3 * PIECE + HALF, S)
         multiply(1, 3)
+        add_bias(1, 3 * PIECE, S)
         store_final(nc.sync, 0, 0, 2 * PIECE)
         scatter(0, 3 * PIECE, S)
         store(0, 2 * PIECE, T)
         store_final(nc.scalar, 1, PIECE, 2 * PIECE)
-        add_bias(1, 3 * PIECE, S)
         scatter(1, 2 * PIECE, S)
         store(1, 2 * PIECE, T)

@@ -47,7 +47,6 @@ def tile_picked_place_lin_bias_srt_l_kernel(tc, xT, w, b, gate, offs, out):
         x_raw = [stage[c][:, MARGIN : MARGIN + PACK * PIECE].rearrange("p (j s) -> p j s", j=PACK) for c in range(PIECES)]
         windows = [keep.tile([P, T], F32, name=f"window{h}") for h in range(ROW_TILES)]
         zero = keep.tile([P, 1], F32, name="zero")
-        warmed = keep.tile([P, 1], F32, name="warmed")
         nc.vector.memset(zero[:], 0.0)
 
         x_rows = xT.rearrange("(p j) s -> p j s", j=PACK)
@@ -60,7 +59,6 @@ def tile_picked_place_lin_bias_srt_l_kernel(tc, xT, w, b, gate, offs, out):
             nc.sync.dma_start(out=gate_rows[:, first:last], in_=gate[0:P, first:last])
 
         nc.scalar.dma_start(out=bias[:], in_=b.rearrange("(p h) o -> p (h o)", p=P))
-        nc.scalar.activation(out=warmed[:], in_=zero[:], func=identity)
         load_x(0)
         nc.sync.dma_start(out=w_raw[:], in_=w.rearrange("(p j) m -> p j m", j=PACK))
         load_x(1)

@@ -17,6 +17,7 @@ P = 128
 PACK = 4
 PIECE = 256
 HALF = PIECE // 2
+CUT = 2 * PIECE + HALF
 PIECES = S // PIECE
 ROW_TILES = N // P
 BANK = 512
@@ -92,7 +93,7 @@ def tile_picked_place_lin_bias_srt_l_kernel(tc, xT, w, b, gate, offs, out):
                 return sums_back[:, first:last]
             return sums_late[:, first - PIECE : last - PIECE]
 
-        final = [keep.tile([P, 2 * PIECE], F32, name="final0"), keep.tile([P, PIECE], F32, name="final1")]
+        final = [keep.tile([P, 3 * PIECE], F32, name="final0"), keep.tile([P, CUT - PIECE], F32, name="final1")]
 
         bias_copies = {
             PIECE: x_grouped[3][:, 0:2].bitcast(F32),
@@ -102,10 +103,12 @@ def tile_picked_place_lin_bias_srt_l_kernel(tc, xT, w, b, gate, offs, out):
         }
 
         products = {}
-        for tenants in (((0, 0),), ((1, 0),), ((0, 1),), ((0, 2),), ((1, 1), (1, 2)), ((0, 3),), ((1, 3),)):
+        for tenants in (((0, 0),), ((1, 0),), ((0, 1),), ((0, 2),), ((1, 1), (1, 2)), ((0, 3),)):
             bank = psum.tile([P, BANK], F32, name="bank%d_%d" % tenants[0])
             for place, tenant in enumerate(tenants):
                 products[tenant] = (bank, PIECE * place)
+
+        products[1, 3] = products[0, 3]
 
         def group_x(copy, c, first, last):
             interleave(copy, x_grouped[c], x_raw[c], first, last)
@@ -162,8 +165,9 @@ def tile_picked_place_lin_bias_srt_l_kernel(tc, xT, w, b, gate, offs, out):
             nc.sync.dma_start(out=out_rows[h, :, first:last], in_=windows[h][:, first:last])
 
         def store_final(queue, h, first, last):
-            nc.scalar.copy(out=final[h][:], in_=windows[h][:, first:last])
-            queue.dma_start(out=out_rows[h, :, first:last], in_=final[h][:])
+            place = final[h][:, first - PIECE * h : last - PIECE * h]
+            nc.scalar.copy(out=place, in_=windows[h][:, first:last])
+            queue.dma_start(out=out_rows[h, :, first:last], in_=place)
 
         group_x(nc.vector.tensor_copy, 0, 0, PIECE)
         quantize_x(0, 0, PIECE)
@@ -202,14 +206,15 @@ def tile_picked_place_lin_bias_srt_l_kernel(tc, xT, w, b, gate, offs, out):
         scatter(0, 2 * PIECE, 3 * PIECE)
 
         add_bias(1, PIECE, 3 * PIECE)
-        scatter(1, PIECE, 2 * PIECE)
+        scatter(1, PIECE, CUT)
         add_bias(0, 3 * PIECE, 3 * PIECE + HALF)
         add_bias(0, 3 * PIECE + HALF, S)
         multiply(1, 3)
+        store_final(nc.sync, 0, 0, PIECE)
+        store_final(nc.sync, 0, PIECE, 3 * PIECE)
         add_bias(1, 3 * PIECE, S)
-        store_final(nc.sync, 0, 0, 2 * PIECE)
         scatter(0, 3 * PIECE, S)
-        store(0, 2 * PIECE, T)
-        store_final(nc.scalar, 1, PIECE, 2 * PIECE)
-        scatter(1, 2 * PIECE, S)
-        store(1, 2 * PIECE, T)
+        store(0, 3 * PIECE, T)
+        store_final(nc.scalar, 1, PIECE, CUT)
+        scatter(1, CUT, S)
+        store(1, CUT, T)

@@ -17,12 +17,9 @@ P = 128
 PACK = 4
 PIECE = 256
 HALF = PIECE // 2
-CUT = 2 * PIECE + HALF
 PIECES = S // PIECE
 ROW_TILES = N // P
 BANK = 512
-SHARED = 8
-MARGIN = PIECE - SHARED
 
 
 def interleave(copy, grouped, raw, first, last):
@@ -34,19 +31,20 @@ def interleave(copy, grouped, raw, first, last):
 
 def tile_picked_place_lin_bias_srt_l_kernel(tc, xT, w, b, gate, offs, out):
     nc = tc.nc
-    identity = mybir.ActivationFunctionType.Identity
+    add, mult = mybir.AluOpType.add, mybir.AluOpType.mult
+    plain = mybir.ActivationFunctionType.Copy
 
     with ExitStack() as ctx:
         keep = ctx.enter_context(tc.tile_pool(name="keep", bufs=1))
         psum = ctx.enter_context(tc.psum_pool(name="psum", bufs=1))
 
         offsets = keep.tile([P, S // 16], U16, name="offsets")
-        bias = keep.tile([P, ROW_TILES], F32, name="bias")
         gate_rows = keep.tile([P, S], F32, name="gate_rows")
         w_raw = keep.tile([P, PACK, N], F32, name="w_raw")
-        stage = [keep.tile([P, MARGIN + PACK * PIECE + MARGIN], F32, name=f"stage{c}") for c in range(PIECES)]
-        x_raw = [stage[c][:, MARGIN : MARGIN + PACK * PIECE].rearrange("p (j s) -> p j s", j=PACK) for c in range(PIECES)]
+        x_raw = [keep.tile([P, PACK, PIECE], F32, name=f"x_raw{c}") for c in range(PIECES)]
         windows = [keep.tile([P, T], F32, name=f"window{h}") for h in range(ROW_TILES)]
+        final1 = keep.tile([P, 2 * PIECE + 8], F32, name="final1")
+        bias = final1[:, 2 * PIECE - 1 : 2 * PIECE + 1]
         zero = keep.tile([P, 1], F32, name="zero")
         nc.vector.memset(zero[:], 0.0)
 
@@ -54,17 +52,17 @@ def tile_picked_place_lin_bias_srt_l_kernel(tc, xT, w, b, gate, offs, out):
         out_rows = out.rearrange("(p h) t -> h p t", h=ROW_TILES)
 
         def load_x(c):
-            nc.sync.dma_start(out=x_raw[c], in_=x_rows[:, :, PIECE * c : PIECE * (c + 1)])
+            nc.sync.dma_start(out=x_raw[c][:], in_=x_rows[:, :, PIECE * c : PIECE * (c + 1)])
 
         def load_gate(first, last):
             nc.sync.dma_start(out=gate_rows[:, first:last], in_=gate[0:P, first:last])
 
-        nc.scalar.dma_start(out=bias[:], in_=b.rearrange("(p h) o -> p (h o)", p=P))
+        nc.scalar.dma_start(out=bias, in_=b.rearrange("(p h) o -> p (h o)", p=P))
         load_x(0)
         nc.sync.dma_start(out=w_raw[:], in_=w.rearrange("(p j) m -> p j m", j=PACK))
         load_x(1)
-        nc.sync.dma_start(offsets[:], offs)
         load_gate(0, PIECE)
+        nc.sync.dma_start(offsets[:], offs)
         load_x(2)
         load_gate(PIECE, 2 * PIECE)
         load_x(3)
@@ -80,35 +78,8 @@ def tile_picked_place_lin_bias_srt_l_kernel(tc, xT, w, b, gate, offs, out):
         x_grouped = [keep.tile([P, PACK * PIECE], BF16, name=f"x_grouped{c}", align_bytes=64) for c in range(PIECES)]
         x_codes = [keep.tile([P, PIECE], U32, name=f"x_codes{c}", align_bytes=64) for c in range(PIECES)]
         x_scales = [keep.tile([P, PIECE], U8, name=f"x_scales{c}", align_bytes=64) for c in range(PIECES)]
-
-        sums_front = [stage[(c + 1) % PIECES][:, :PIECE] for c in range(PIECES)]
-        sums_back = stage[1][:, 2 * MARGIN + (PACK - 1) * PIECE :]
-        sums_late = keep.tile([P, S - PIECE], F32, name="sums_late")
-
-        def sums(h, first, last):
-            if h == 0:
-                c = first // PIECE
-                return sums_front[c][:, first - PIECE * c : last - PIECE * c]
-            if first < PIECE:
-                return sums_back[:, first:last]
-            return sums_late[:, first - PIECE : last - PIECE]
-
-        final = [keep.tile([P, 3 * PIECE], F32, name="final0"), keep.tile([P, CUT - PIECE], F32, name="final1")]
-
-        bias_copies = {
-            PIECE: x_grouped[3][:, 0:2].bitcast(F32),
-            2 * PIECE: sums_late[:, 0:1],
-            3 * PIECE: final[0][:, 0:1],
-            3 * PIECE + HALF: final[1][:, 0:1],
-        }
-
-        products = {}
-        for tenants in (((0, 0),), ((1, 0),), ((0, 1),), ((0, 2),), ((1, 1), (1, 2)), ((0, 3),)):
-            bank = psum.tile([P, BANK], F32, name="bank%d_%d" % tenants[0])
-            for place, tenant in enumerate(tenants):
-                products[tenant] = (bank, PIECE * place)
-
-        products[1, 3] = products[0, 3]
+        results = [keep.tile([P, S], F32, name=f"results{h}") for h in range(ROW_TILES)]
+        banks = [[psum.tile([P, BANK], F32, name=f"bank{h}_{c}") for c in range(PIECES)] for h in range(ROW_TILES)]
 
         def group_x(copy, c, first, last):
             interleave(copy, x_grouped[c], x_raw[c], first, last)
@@ -124,97 +95,77 @@ def tile_picked_place_lin_bias_srt_l_kernel(tc, xT, w, b, gate, offs, out):
                 in_=w_grouped[:, PACK * P * h : PACK * P * (h + 1)],
             )
 
-        def quantize_x(c, first, last):
-            nc.vector.quantize_mx(
-                out=x_codes[c][:, first:last].bitcast(FP8X4),
-                scales=x_scales[c][:, first:last],
-                in_=x_grouped[c][:, PACK * first : PACK * last],
+        def quantize_x(c):
+            nc.vector.quantize_mx(out=x_codes[c][:].bitcast(FP8X4), scales=x_scales[c][:], in_=x_grouped[c][:])
+
+        def multiply(c):
+            for h in range(ROW_TILES):
+                nc.tensor.matmul_mx(
+                    out=banks[h][c][:, :PIECE],
+                    lhsT=w_codes[h][:].bitcast(FP8X4),
+                    lhsT_scale=w_scales[h][:],
+                    rhs=x_codes[c][:].bitcast(FP8X4),
+                    rhs_scale=x_scales[c][:],
+                    start=True,
+                    stop=True,
+                )
+
+        def finish(h, c):
+            columns = slice(PIECE * c, PIECE * (c + 1))
+            nc.vector.scalar_tensor_tensor(
+                out=results[h][:, columns],
+                in0=banks[h][c][:, :PIECE],
+                scalar=bias[:, h : h + 1],
+                in1=gate_rows[:, columns],
+                op0=add,
+                op1=mult,
             )
 
-        def multiply(h, c):
-            bank, column = products[h, c]
-            nc.tensor.matmul_mx(
-                out=bank[:, column : column + PIECE],
-                lhsT=w_codes[h][:].bitcast(FP8X4),
-                lhsT_scale=w_scales[h][:],
-                rhs=x_codes[c][:].bitcast(FP8X4),
-                rhs_scale=x_scales[c][:],
-                start=True,
-                stop=True,
-            )
+        def places(h, first, last):
+            return windows[h][:].indirect(offsets[:, first // 16 : last // 16])
 
-        def add_bias(h, first, last):
-            bank, column = products[h, first // PIECE]
-            column = column + first % PIECE
-            nc.scalar.activation(
-                out=sums(h, first, last),
-                in_=bank[:, column : column + last - first],
-                func=identity,
-                bias=bias_copies[first] if h == 0 and first in bias_copies else bias[:, h : h + 1],
-            )
+        def scatter(h, c):
+            first, last = PIECE * c, PIECE * (c + 1)
+            nc.scalar.activation(places(h, first, last), results[h][:, first:last], plain)
 
-        def scatter(h, first, last):
-            nc.vector.tensor_tensor(
-                windows[h][:].indirect(offsets[:, first // 16 : last // 16]),
-                sums(h, first, last),
-                gate_rows[:, first:last],
-                mybir.AluOpType.mult,
-            )
-
-        def store(h, first, last):
-            nc.sync.dma_start(out=out_rows[h, :, first:last], in_=windows[h][:, first:last])
-
-        def store_final(queue, h, first, last):
-            place = final[h][:, first - PIECE * h : last - PIECE * h]
-            nc.scalar.copy(out=place, in_=windows[h][:, first:last])
-            queue.dma_start(out=out_rows[h, :, first:last], in_=place)
+        def store(h, first, last, source):
+            nc.sync.dma_start(out=out_rows[h, :, first:last], in_=source)
 
         group_x(nc.vector.tensor_copy, 0, 0, PIECE)
-        quantize_x(0, 0, PIECE)
+        quantize_x(0)
         group_w(nc.vector.tensor_copy, 0)
         group_w(nc.scalar.copy, 1)
-        for place in bias_copies.values():
-            nc.scalar.copy(out=place, in_=bias[:, 0:1])
-        for h in range(ROW_TILES):
-            quantize_w(h)
-            multiply(h, 0)
-
+        quantize_w(0)
+        quantize_w(1)
+        multiply(0)
+        group_x(nc.scalar.copy, 1, 0, HALF)
         group_x(nc.vector.tensor_copy, 1, HALF, PIECE)
-        group_x(nc.vector.tensor_copy, 1, 0, HALF)
-        add_bias(1, 0, PIECE)
-        add_bias(0, 0, PIECE)
-        quantize_x(1, HALF, PIECE)
-        quantize_x(1, 0, HALF)
-        multiply(0, 1)
-        scatter(1, 0, PIECE)
-        scatter(0, 0, PIECE)
-        store(1, 0, PIECE)
-
-        group_x(nc.scalar.copy, 2, 0, PIECE)
-        quantize_x(2, 0, PIECE)
-        multiply(0, 2)
-        add_bias(0, PIECE, 2 * PIECE)
-        scatter(0, PIECE, 2 * PIECE)
-        multiply(1, 1)
-        multiply(1, 2)
-
-        group_x(nc.vector.tensor_copy, 3, HALF, PIECE)
-        group_x(nc.scalar.copy, 3, 0, HALF)
-        quantize_x(3, 0, PIECE)
-        multiply(0, 3)
-        add_bias(0, 2 * PIECE, 3 * PIECE)
-        scatter(0, 2 * PIECE, 3 * PIECE)
-
-        add_bias(1, PIECE, 3 * PIECE)
-        scatter(1, PIECE, CUT)
-        add_bias(0, 3 * PIECE, 3 * PIECE + HALF)
-        add_bias(0, 3 * PIECE + HALF, S)
-        multiply(1, 3)
-        store_final(nc.sync, 0, 0, PIECE)
-        store_final(nc.sync, 0, PIECE, 3 * PIECE)
-        add_bias(1, 3 * PIECE, S)
-        scatter(0, 3 * PIECE, S)
-        store(0, 3 * PIECE, T)
-        store_final(nc.scalar, 1, PIECE, CUT)
-        scatter(1, CUT, S)
-        store(1, CUT, T)
+        finish(0, 0)
+        scatter(0, 0)
+        quantize_x(1)
+        multiply(1)
+        finish(1, 0)
+        scatter(1, 0)
+        group_x(nc.vector.tensor_copy, 2, 0, PIECE)
+        finish(0, 1)
+        scatter(0, 1)
+        quantize_x(2)
+        multiply(2)
+        finish(1, 1)
+        scatter(1, 1)
+        group_x(nc.vector.tensor_copy, 3, 0, PIECE)
+        nc.vector.tensor_copy(out=gate_rows[:, : 2 * PIECE], in_=windows[0][:, : 2 * PIECE])
+        store(0, 0, 2 * PIECE, gate_rows[:, : 2 * PIECE])
+        finish(0, 2)
+        scatter(0, 2)
+        quantize_x(3)
+        multiply(3)
+        finish(1, 2)
+        finish(0, 3)
+        scatter(0, 3)
+        store(0, 2 * PIECE, T, windows[0][:, 2 * PIECE :])
+        finish(1, 3)
+        nc.vector.tensor_copy(out=final1[:, : 2 * PIECE], in_=windows[1][:, : 2 * PIECE])
+        nc.scalar.dma_start(out=out_rows[1, :, : 2 * PIECE], in_=final1[:, : 2 * PIECE])
+        nc.vector.tensor_copy(places(1, 2 * PIECE, S), results[1][:, 2 * PIECE :])
+        store(1, 2 * PIECE, T, windows[1][:, 2 * PIECE :])

@@ -19,6 +19,8 @@ PIECE = 256
 HALF = PIECE // 2
 PIECES = S // PIECE
 ROW_TILES = N // P
+STAGED = 2 * PIECE
+MARGIN = STAGED - 8
 BANK = 512
 
 
@@ -41,10 +43,13 @@ def tile_picked_place_lin_bias_srt_l_kernel(tc, xT, w, b, gate, offs, out):
         offsets = keep.tile([P, S // 16], U16, name="offsets")
         gate_rows = keep.tile([P, S], F32, name="gate_rows")
         w_raw = keep.tile([P, PACK, N], F32, name="w_raw")
-        x_raw = [keep.tile([P, PACK, PIECE], F32, name=f"x_raw{c}") for c in range(PIECES)]
+        last = keep.tile([P, MARGIN + PACK * PIECE + MARGIN], F32, name="last")
+        x_raw = [keep.tile([P, PACK, PIECE], F32, name=f"x_raw{c}")[:] for c in range(PIECES - 1)]
+        x_raw.append(last[:, MARGIN : MARGIN + PACK * PIECE].rearrange("p (j s) -> p j s", j=PACK))
+        final = [last[:, :STAGED], last[:, 2 * MARGIN + PACK * PIECE - STAGED :]]
         windows = [keep.tile([P, T], F32, name=f"window{h}") for h in range(ROW_TILES)]
-        final1 = keep.tile([P, 2 * PIECE + 8], F32, name="final1")
-        bias = final1[:, 2 * PIECE - 1 : 2 * PIECE + 1]
+        late = keep.tile([P, 2 * PIECE], F32, name="late")
+        bias = late[:, PIECE - 1 : PIECE + 1]
         zero = keep.tile([P, 1], F32, name="zero")
         nc.vector.memset(zero[:], 0.0)
 
@@ -52,7 +57,7 @@ def tile_picked_place_lin_bias_srt_l_kernel(tc, xT, w, b, gate, offs, out):
         out_rows = out.rearrange("(p h) t -> h p t", h=ROW_TILES)
 
         def load_x(c):
-            nc.sync.dma_start(out=x_raw[c][:], in_=x_rows[:, :, PIECE * c : PIECE * (c + 1)])
+            nc.sync.dma_start(out=x_raw[c], in_=x_rows[:, :, PIECE * c : PIECE * (c + 1)])
 
         def load_gate(first, last):
             nc.sync.dma_start(out=gate_rows[:, first:last], in_=gate[0:P, first:last])
@@ -131,6 +136,10 @@ def tile_picked_place_lin_bias_srt_l_kernel(tc, xT, w, b, gate, offs, out):
         def store(h, first, last, source):
             nc.sync.dma_start(out=out_rows[h, :, first:last], in_=source)
 
+        def stage(h, first, last, place):
+            nc.vector.tensor_copy(out=place, in_=windows[h][:, first:last])
+            store(h, first, last, place)
+
         group_x(nc.vector.tensor_copy, 0, 0, PIECE)
         quantize_x(0)
         group_w(nc.vector.tensor_copy, 0)
@@ -153,19 +162,21 @@ def tile_picked_place_lin_bias_srt_l_kernel(tc, xT, w, b, gate, offs, out):
         multiply(2)
         finish(1, 1)
         scatter(1, 1)
-        group_x(nc.vector.tensor_copy, 3, 0, PIECE)
-        nc.vector.tensor_copy(out=gate_rows[:, : 2 * PIECE], in_=windows[0][:, : 2 * PIECE])
-        store(0, 0, 2 * PIECE, gate_rows[:, : 2 * PIECE])
+        group_x(nc.vector.tensor_copy, 3, 0, HALF)
+        group_x(nc.vector.tensor_copy, 3, HALF, PIECE)
+        stage(0, 0, STAGED, final[0])
         finish(0, 2)
         scatter(0, 2)
         quantize_x(3)
         multiply(3)
         finish(1, 2)
+        stage(1, 0, STAGED, final[1])
+        scatter(1, 2)
         finish(0, 3)
-        scatter(0, 3)
-        store(0, 2 * PIECE, T, windows[0][:, 2 * PIECE :])
         finish(1, 3)
-        nc.vector.tensor_copy(out=final1[:, : 2 * PIECE], in_=windows[1][:, : 2 * PIECE])
-        nc.scalar.dma_start(out=out_rows[1, :, : 2 * PIECE], in_=final1[:, : 2 * PIECE])
-        nc.vector.tensor_copy(places(1, 2 * PIECE, S), results[1][:, 2 * PIECE :])
-        store(1, 2 * PIECE, T, windows[1][:, 2 * PIECE :])
+        stage(0, STAGED, STAGED + PIECE, late[:, :PIECE])
+        scatter(0, 3)
+        nc.scalar.dma_start(out=out_rows[0, :, 3 * PIECE :], in_=windows[0][:, 3 * PIECE :])
+        stage(1, STAGED, STAGED + PIECE, late[:, PIECE:])
+        nc.vector.tensor_copy(places(1, 3 * PIECE, S), results[1][:, 3 * PIECE :])
+        store(1, 3 * PIECE, T, windows[1][:, 3 * PIECE :])

@@ -20,7 +20,7 @@ HALF = PIECE // 2
 PIECES = S // PIECE
 ROW_TILES = N // P
 STAGED = 2 * PIECE
-MARGIN = STAGED - 8
+SHARED = 8
 BANK = 512
 
 
@@ -43,13 +43,11 @@ def tile_picked_place_lin_bias_srt_l_kernel(tc, xT, w, b, gate, offs, out):
         offsets = keep.tile([P, S // 16], U16, name="offsets")
         gate_rows = keep.tile([P, S], F32, name="gate_rows")
         w_raw = keep.tile([P, PACK, N], F32, name="w_raw")
-        last = keep.tile([P, MARGIN + PACK * PIECE + MARGIN], F32, name="last")
+        last = keep.tile([P, PIECE - SHARED + PACK * PIECE + STAGED - SHARED], F32, name="last")
         x_raw = [keep.tile([P, PACK, PIECE], F32, name=f"x_raw{c}")[:] for c in range(PIECES - 1)]
-        x_raw.append(last[:, MARGIN : MARGIN + PACK * PIECE].rearrange("p (j s) -> p j s", j=PACK))
-        final = [last[:, :STAGED], last[:, 2 * MARGIN + PACK * PIECE - STAGED :]]
+        x_raw.append(last[:, PIECE - SHARED : PIECE - SHARED + PACK * PIECE].rearrange("p (j s) -> p j s", j=PACK))
         windows = [keep.tile([P, T], F32, name=f"window{h}") for h in range(ROW_TILES)]
-        late = keep.tile([P, 2 * PIECE], F32, name="late")
-        bias = late[:, PIECE - 1 : PIECE + 1]
+        bias = keep.tile([P, ROW_TILES], F32, name="bias")
         zero = keep.tile([P, 1], F32, name="zero")
         nc.vector.memset(zero[:], 0.0)
 
@@ -62,16 +60,16 @@ def tile_picked_place_lin_bias_srt_l_kernel(tc, xT, w, b, gate, offs, out):
         def load_gate(first, last):
             nc.sync.dma_start(out=gate_rows[:, first:last], in_=gate[0:P, first:last])
 
-        nc.scalar.dma_start(out=bias, in_=b.rearrange("(p h) o -> p (h o)", p=P))
+        nc.scalar.dma_start(out=bias[:], in_=b.rearrange("(p h) o -> p (h o)", p=P))
         load_x(0)
         nc.sync.dma_start(out=w_raw[:], in_=w.rearrange("(p j) m -> p j m", j=PACK))
         load_x(1)
         load_gate(0, PIECE)
         nc.sync.dma_start(offsets[:], offs)
         load_x(2)
-        load_gate(PIECE, 2 * PIECE)
+        load_gate(PIECE, 3 * PIECE)
         load_x(3)
-        load_gate(2 * PIECE, S)
+        load_gate(3 * PIECE, S)
 
         for h in range(ROW_TILES):
             for first in (0, T // 2):
@@ -84,6 +82,13 @@ def tile_picked_place_lin_bias_srt_l_kernel(tc, xT, w, b, gate, offs, out):
         x_codes = [keep.tile([P, PIECE], U32, name=f"x_codes{c}", align_bytes=64) for c in range(PIECES)]
         x_scales = [keep.tile([P, PIECE], U8, name=f"x_scales{c}", align_bytes=64) for c in range(PIECES)]
         results = [keep.tile([P, S], F32, name=f"results{h}") for h in range(ROW_TILES)]
+        final = [last[:, PIECE + PACK * PIECE - 2 * SHARED :], x_grouped[PIECES - 1][:].bitcast(F32)]
+
+        def result(h, first, last_entry):
+            if (h, first) == (0, 2 * PIECE):
+                return last[:, :PIECE]
+            return results[h][:, first:last_entry]
+
         banks = [[psum.tile([P, BANK], F32, name=f"bank{h}_{c}") for c in range(PIECES)] for h in range(ROW_TILES)]
 
         def group_x(copy, c, first, last):
@@ -118,7 +123,7 @@ def tile_picked_place_lin_bias_srt_l_kernel(tc, xT, w, b, gate, offs, out):
         def finish(h, c):
             columns = slice(PIECE * c, PIECE * (c + 1))
             nc.vector.scalar_tensor_tensor(
-                out=results[h][:, columns],
+                out=result(h, columns.start, columns.stop),
                 in0=banks[h][c][:, :PIECE],
                 scalar=bias[:, h : h + 1],
                 in1=gate_rows[:, columns],
@@ -131,7 +136,7 @@ def tile_picked_place_lin_bias_srt_l_kernel(tc, xT, w, b, gate, offs, out):
 
         def scatter(h, c):
             first, last = PIECE * c, PIECE * (c + 1)
-            nc.scalar.activation(places(h, first, last), results[h][:, first:last], plain)
+            nc.scalar.activation(places(h, first, last), result(h, first, last), plain)
 
         def store(h, first, last, source):
             nc.sync.dma_start(out=out_rows[h, :, first:last], in_=source)
@@ -164,19 +169,21 @@ def tile_picked_place_lin_bias_srt_l_kernel(tc, xT, w, b, gate, offs, out):
         scatter(1, 1)
         group_x(nc.vector.tensor_copy, 3, 0, HALF)
         group_x(nc.vector.tensor_copy, 3, HALF, PIECE)
-        stage(0, 0, STAGED, final[0])
         finish(0, 2)
+        stage(0, 0, STAGED, final[0])
         scatter(0, 2)
+        nc.scalar.activation(
+            out=results[1][:, 2 * PIECE : 3 * PIECE],
+            in_=banks[1][2][:, :PIECE],
+            func=mybir.ActivationFunctionType.Identity,
+            bias=bias[:, 1:2],
+        )
         quantize_x(3)
         multiply(3)
-        finish(1, 2)
         stage(1, 0, STAGED, final[1])
-        scatter(1, 2)
         finish(0, 3)
-        finish(1, 3)
-        stage(0, STAGED, STAGED + PIECE, late[:, :PIECE])
         scatter(0, 3)
-        nc.scalar.dma_start(out=out_rows[0, :, 3 * PIECE :], in_=windows[0][:, 3 * PIECE :])
-        stage(1, STAGED, STAGED + PIECE, late[:, PIECE:])
-        nc.vector.tensor_copy(places(1, 3 * PIECE, S), results[1][:, 3 * PIECE :])
-        store(1, 3 * PIECE, T, windows[1][:, 3 * PIECE :])
+        nc.scalar.dma_start(out=out_rows[0, :, STAGED:], in_=windows[0][:, STAGED:])
+        nc.vector.tensor_scalar_add(out=results[1][:, 3 * PIECE :], in0=banks[1][3][:, :PIECE], scalar1=bias[:, 1:2])
+        nc.vector.tensor_tensor(places(1, STAGED, S), results[1][:, STAGED:], gate_rows[:, STAGED:], mult)
+        store(1, STAGED, T, windows[1][:, STAGED:])

@@ -131,6 +131,14 @@ def tile_picked_place_lin_bias_srt_l_kernel(tc, xT, w, b, gate, offs, out):
                 op1=mult,
             )
 
+        def add_bias(h, c):
+            nc.scalar.activation(
+                out=results[h][:, PIECE * c : PIECE * (c + 1)],
+                in_=banks[h][c][:, :PIECE],
+                func=mybir.ActivationFunctionType.Identity,
+                bias=bias[:, h : h + 1],
+            )
+
         def places(h, first, last):
             return windows[h][:].indirect(offsets[:, first // 16 : last // 16])
 
@@ -172,18 +180,13 @@ def tile_picked_place_lin_bias_srt_l_kernel(tc, xT, w, b, gate, offs, out):
         finish(0, 2)
         stage(0, 0, STAGED, final[0])
         scatter(0, 2)
-        nc.scalar.activation(
-            out=results[1][:, 2 * PIECE : 3 * PIECE],
-            in_=banks[1][2][:, :PIECE],
-            func=mybir.ActivationFunctionType.Identity,
-            bias=bias[:, 1:2],
-        )
+        add_bias(1, 2)
         quantize_x(3)
         multiply(3)
         stage(1, 0, STAGED, final[1])
         finish(0, 3)
+        add_bias(1, 3)
         scatter(0, 3)
-        nc.scalar.dma_start(out=out_rows[0, :, STAGED:], in_=windows[0][:, STAGED:])
-        nc.vector.tensor_scalar_add(out=results[1][:, 3 * PIECE :], in0=banks[1][3][:, :PIECE], scalar1=bias[:, 1:2])
+        store(0, STAGED, T, windows[0][:, STAGED:])
         nc.vector.tensor_tensor(places(1, STAGED, S), results[1][:, STAGED:], gate_rows[:, STAGED:], mult)
         store(1, STAGED, T, windows[1][:, STAGED:])

@@ -16,7 +16,7 @@ FP8X4 = mybir.dt.float8_e4m3fn_x4
 P = 128
 PACK = 4
 PIECE = 256
-HALF = PIECE // 2
+SHARE = PIECE // 4
 PIECES = S // PIECE
 ROW_TILES = N // P
 STAGED = 2 * PIECE
@@ -43,9 +43,9 @@ def tile_picked_place_lin_bias_srt_l_kernel(tc, xT, w, b, gate, offs, out):
         offsets = keep.tile([P, S // 16], U16, name="offsets")
         gate_rows = keep.tile([P, S], F32, name="gate_rows")
         w_raw = keep.tile([P, PACK, N], F32, name="w_raw")
-        last = keep.tile([P, PIECE - SHARED + PACK * PIECE + STAGED - SHARED], F32, name="last")
+        last = keep.tile([P, PACK * PIECE + STAGED - SHARED], F32, name="last")
         x_raw = [keep.tile([P, PACK, PIECE], F32, name=f"x_raw{c}")[:] for c in range(PIECES - 1)]
-        x_raw.append(last[:, PIECE - SHARED : PIECE - SHARED + PACK * PIECE].rearrange("p (j s) -> p j s", j=PACK))
+        x_raw.append(last[:, : PACK * PIECE].rearrange("p (j s) -> p j s", j=PACK))
         windows = [keep.tile([P, T], F32, name=f"window{h}") for h in range(ROW_TILES)]
         bias = keep.tile([P, ROW_TILES], F32, name="bias")
         zero = keep.tile([P, 1], F32, name="zero")
@@ -67,8 +67,9 @@ def tile_picked_place_lin_bias_srt_l_kernel(tc, xT, w, b, gate, offs, out):
         load_gate(0, PIECE)
         nc.sync.dma_start(offsets[:], offs)
         load_x(2)
-        load_gate(PIECE, 3 * PIECE)
+        load_gate(PIECE, 2 * PIECE)
         load_x(3)
+        load_gate(2 * PIECE, 3 * PIECE)
         load_gate(3 * PIECE, S)
 
         for h in range(ROW_TILES):
@@ -82,12 +83,7 @@ def tile_picked_place_lin_bias_srt_l_kernel(tc, xT, w, b, gate, offs, out):
         x_codes = [keep.tile([P, PIECE], U32, name=f"x_codes{c}", align_bytes=64) for c in range(PIECES)]
         x_scales = [keep.tile([P, PIECE], U8, name=f"x_scales{c}", align_bytes=64) for c in range(PIECES)]
         results = [keep.tile([P, S], F32, name=f"results{h}") for h in range(ROW_TILES)]
-        final = [last[:, PIECE + PACK * PIECE - 2 * SHARED :], x_grouped[PIECES - 1][:].bitcast(F32)]
-
-        def result(h, first, last_entry):
-            if (h, first) == (0, 2 * PIECE):
-                return last[:, :PIECE]
-            return results[h][:, first:last_entry]
+        final = [last[:, PACK * PIECE - SHARED :], x_grouped[PIECES - 1][:].bitcast(F32)]
 
         banks = [[psum.tile([P, BANK], F32, name=f"bank{h}_{c}") for c in range(PIECES)] for h in range(ROW_TILES)]
 
@@ -123,7 +119,7 @@ def tile_picked_place_lin_bias_srt_l_kernel(tc, xT, w, b, gate, offs, out):
         def finish(h, c):
             columns = slice(PIECE * c, PIECE * (c + 1))
             nc.vector.scalar_tensor_tensor(
-                out=result(h, columns.start, columns.stop),
+                out=results[h][:, columns],
                 in0=banks[h][c][:, :PIECE],
                 scalar=bias[:, h : h + 1],
                 in1=gate_rows[:, columns],
@@ -144,7 +140,7 @@ def tile_picked_place_lin_bias_srt_l_kernel(tc, xT, w, b, gate, offs, out):
 
         def scatter(h, c):
             first, last = PIECE * c, PIECE * (c + 1)
-            nc.scalar.activation(places(h, first, last), result(h, first, last), plain)
+            nc.scalar.activation(places(h, first, last), results[h][:, first:last], plain)
 
         def store(h, first, last, source):
             nc.sync.dma_start(out=out_rows[h, :, first:last], in_=source)
@@ -160,8 +156,8 @@ def tile_picked_place_lin_bias_srt_l_kernel(tc, xT, w, b, gate, offs, out):
         quantize_w(0)
         quantize_w(1)
         multiply(0)
-        group_x(nc.scalar.copy, 1, 0, HALF)
-        group_x(nc.vector.tensor_copy, 1, HALF, PIECE)
+        group_x(nc.scalar.copy, 1, 0, SHARE)
+        group_x(nc.vector.tensor_copy, 1, SHARE, PIECE)
         finish(0, 0)
         scatter(0, 0)
         quantize_x(1)
@@ -175,8 +171,7 @@ def tile_picked_place_lin_bias_srt_l_kernel(tc, xT, w, b, gate, offs, out):
         multiply(2)
         finish(1, 1)
         scatter(1, 1)
-        group_x(nc.vector.tensor_copy, 3, 0, HALF)
-        group_x(nc.vector.tensor_copy, 3, HALF, PIECE)
+        group_x(nc.vector.tensor_copy, 3, 0, PIECE)
         finish(0, 2)
         stage(0, 0, STAGED, final[0])
         scatter(0, 2)
@@ -185,8 +180,8 @@ def tile_picked_place_lin_bias_srt_l_kernel(tc, xT, w, b, gate, offs, out):
         multiply(3)
         stage(1, 0, STAGED, final[1])
         finish(0, 3)
-        add_bias(1, 3)
         scatter(0, 3)
         store(0, STAGED, T, windows[0][:, STAGED:])
+        nc.vector.tensor_scalar_add(out=results[1][:, 3 * PIECE :], in0=banks[1][3][:, :PIECE], scalar1=bias[:, 1:2])
         nc.vector.tensor_tensor(places(1, STAGED, S), results[1][:, STAGED:], gate_rows[:, STAGED:], mult)
         store(1, STAGED, T, windows[1][:, STAGED:])

@@ -16,7 +16,7 @@ FP8X4 = mybir.dt.float8_e4m3fn_x4
 P = 128
 PACK = 4
 PIECE = 256
-SHARE = PIECE // 4
+SHARE = PIECE // 2
 PIECES = S // PIECE
 ROW_TILES = N // P
 STAGED = 2 * PIECE
@@ -127,14 +127,6 @@ def tile_picked_place_lin_bias_srt_l_kernel(tc, xT, w, b, gate, offs, out):
                 op1=mult,
             )
 
-        def add_bias(h, c):
-            nc.scalar.activation(
-                out=results[h][:, PIECE * c : PIECE * (c + 1)],
-                in_=banks[h][c][:, :PIECE],
-                func=mybir.ActivationFunctionType.Identity,
-                bias=bias[:, h : h + 1],
-            )
-
         def places(h, first, last):
             return windows[h][:].indirect(offsets[:, first // 16 : last // 16])
 
@@ -175,13 +167,13 @@ def tile_picked_place_lin_bias_srt_l_kernel(tc, xT, w, b, gate, offs, out):
         finish(0, 2)
         stage(0, 0, STAGED, final[0])
         scatter(0, 2)
-        add_bias(1, 2)
         quantize_x(3)
         multiply(3)
+        finish(1, 2)
         stage(1, 0, STAGED, final[1])
         finish(0, 3)
         scatter(0, 3)
         store(0, STAGED, T, windows[0][:, STAGED:])
-        nc.vector.tensor_scalar_add(out=results[1][:, 3 * PIECE :], in0=banks[1][3][:, :PIECE], scalar1=bias[:, 1:2])
-        nc.vector.tensor_tensor(places(1, STAGED, S), results[1][:, STAGED:], gate_rows[:, STAGED:], mult)
+        finish(1, 3)
+        nc.vector.tensor_copy(places(1, STAGED, S), results[1][:, STAGED:])
         store(1, STAGED, T, windows[1][:, STAGED:])

@@ -80,7 +80,7 @@ def tile_picked_place_lin_bias_srt_l_kernel(tc, xT, w, b, gate, offs, out):
         w_codes = [keep.tile([P, P], U32, name=f"w_codes{h}", align_bytes=64) for h in range(ROW_TILES)]
         w_scales = [keep.tile([P, P], U8, name=f"w_scales{h}", align_bytes=64) for h in range(ROW_TILES)]
         x_grouped = [keep.tile([P, PACK * PIECE], BF16, name=f"x_grouped{c}", align_bytes=64) for c in range(PIECES)]
-        x_codes = [keep.tile([P, PIECE], U32, name=f"x_codes{c}", align_bytes=64) for c in range(PIECES)]
+        x_codes = [keep.tile([P, PIECE], U32, name=f"x_codes{c}", tag=f"codes{c}", align_bytes=64) for c in range(PIECES)]
         x_scales = [keep.tile([P, PIECE], U8, name=f"x_scales{c}", align_bytes=64) for c in range(PIECES)]
         results = [keep.tile([P, S], F32, name=f"results{h}") for h in range(ROW_TILES)]
         final = [last[:, PACK * PIECE - SHARED :], x_grouped[PIECES - 1][:].bitcast(F32)]
@@ -137,9 +137,8 @@ def tile_picked_place_lin_bias_srt_l_kernel(tc, xT, w, b, gate, offs, out):
         def store(h, first, last, source):
             nc.sync.dma_start(out=out_rows[h, :, first:last], in_=source)
 
-        def stage(h, first, last, place):
-            nc.vector.tensor_copy(out=place, in_=windows[h][:, first:last])
-            store(h, first, last, place)
+        def stage(copy, h, first, last, place):
+            copy(out=place, in_=windows[h][:, first:last])
 
         group_x(nc.vector.tensor_copy, 0, 0, PIECE)
         quantize_x(0)
@@ -165,15 +164,21 @@ def tile_picked_place_lin_bias_srt_l_kernel(tc, xT, w, b, gate, offs, out):
         scatter(1, 1)
         group_x(nc.vector.tensor_copy, 3, 0, PIECE)
         finish(0, 2)
-        stage(0, 0, STAGED, final[0])
+        stage(nc.vector.tensor_copy, 0, 0, STAGED, final[0])
+        store(0, 0, STAGED, final[0])
         scatter(0, 2)
         quantize_x(3)
         multiply(3)
         finish(1, 2)
-        stage(1, 0, STAGED, final[1])
+        stage(nc.vector.tensor_copy, 1, 0, PIECE, final[1][:, :PIECE])
+        stage(nc.scalar.copy, 1, PIECE, STAGED, final[1][:, PIECE:])
+        store(1, 0, STAGED, final[1])
         finish(0, 3)
+        late = keep.tile([P, PIECE], F32, name="late", tag=f"codes{PIECES - 1}", align_bytes=64)
+        stage(nc.vector.tensor_copy, 0, STAGED, STAGED + PIECE, late[:])
+        store(0, STAGED, STAGED + PIECE, late[:])
         scatter(0, 3)
-        store(0, STAGED, T, windows[0][:, STAGED:])
+        store(0, STAGED + PIECE, T, windows[0][:, STAGED + PIECE :])
         finish(1, 3)
         nc.vector.tensor_copy(places(1, STAGED, S), results[1][:, STAGED:])
         store(1, STAGED, T, windows[1][:, STAGED:])

@@ -19,8 +19,10 @@ PIECE = 256
 SHARE = PIECE // 2
 PIECES = S // PIECE
 ROW_TILES = N // P
+CLEAR = 768
 STAGED = 2 * PIECE
 SHARED = 8
+QUADRANT = 32
 BANK = 512
 
 
@@ -48,8 +50,29 @@ def tile_picked_place_lin_bias_srt_l_kernel(tc, xT, w, b, gate, offs, out):
         x_raw.append(last[:, : PACK * PIECE].rearrange("p (j s) -> p j s", j=PACK))
         windows = [keep.tile([P, T], F32, name=f"window{h}") for h in range(ROW_TILES)]
         bias = keep.tile([P, ROW_TILES], F32, name="bias")
+        bias_row = keep.tile([1, N], F32, name="bias_row")
+        bias_rows = keep.tile([P, N], F32, name="bias_rows")
         zero = keep.tile([P, 1], F32, name="zero")
-        nc.vector.memset(zero[:], 0.0)
+        ones = keep.tile([P, P], F32, name="ones")
+        column = keep.tile([P, P], F32, name="column", align_bytes=64)
+        row = keep.tile([P, QUADRANT], F32, name="row", align_bytes=64)
+        number = keep.tile([P, 1], F32, name="number")
+        identity = keep.tile([P, P], F32, name="identity")
+        nc.gpsimd.memset(zero[:], 0.0)
+        nc.gpsimd.memset(ones[:], 1.0)
+        for first in range(0, P, QUADRANT):
+            nc.gpsimd.memset(number[first : first + QUADRANT, :], float(first))
+        nc.gpsimd.memset(bias_rows[:], 0.0)
+        nc.vector.tensor_tensor_scan(column[:], ones[:], ones[:], 0.0, mult, add)
+        nc.vector.transpose(row[:], column[:, :QUADRANT])
+        nc.vector.tensor_scalar(
+            out=identity[:],
+            in0=column[:],
+            scalar1=row[:, 0:1],
+            scalar2=number[:],
+            op0=mybir.AluOpType.subtract,
+            op1=mybir.AluOpType.is_equal,
+        )
 
         x_rows = xT.rearrange("(p j) s -> p j s", j=PACK)
         out_rows = out.rearrange("(p h) t -> h p t", h=ROW_TILES)
@@ -60,8 +83,8 @@ def tile_picked_place_lin_bias_srt_l_kernel(tc, xT, w, b, gate, offs, out):
         def load_gate(first, last):
             nc.sync.dma_start(out=gate_rows[:, first:last], in_=gate[0:P, first:last])
 
-        nc.scalar.dma_start(out=bias[:], in_=b.rearrange("(p h) o -> p (h o)", p=P))
         load_x(0)
+        nc.sync.dma_start(out=bias_row[:], in_=b.rearrange("m o -> o m"))
         nc.sync.dma_start(out=w_raw[:], in_=w.rearrange("(p j) m -> p j m", j=PACK))
         load_x(1)
         load_gate(0, PIECE)
@@ -72,9 +95,9 @@ def tile_picked_place_lin_bias_srt_l_kernel(tc, xT, w, b, gate, offs, out):
         load_gate(2 * PIECE, 3 * PIECE)
         load_gate(3 * PIECE, S)
 
-        for h in range(ROW_TILES):
-            for first in (0, T // 2):
-                nc.vector.tensor_copy(out=windows[h][:, first : first + T // 2], in_=zero[:].to_broadcast([P, T // 2]))
+        for h, first, end in ((0, 0, T // 2), (0, T // 2, T), (1, 0, CLEAR)):
+            nc.vector.tensor_copy(out=windows[h][:, first:end], in_=zero[:].to_broadcast([P, end - first]))
+        nc.scalar.copy(out=windows[1][:, CLEAR:], in_=zero[:].to_broadcast([P, T - CLEAR]))
 
         w_grouped = keep.tile([P, PACK * N], BF16, name="w_grouped", align_bytes=64)
         w_codes = [keep.tile([P, P], U32, name=f"w_codes{h}", align_bytes=64) for h in range(ROW_TILES)]
@@ -86,6 +109,11 @@ def tile_picked_place_lin_bias_srt_l_kernel(tc, xT, w, b, gate, offs, out):
         final = [last[:, PACK * PIECE - SHARED :], x_grouped[PIECES - 1][:].bitcast(F32)]
 
         banks = [[psum.tile([P, BANK], F32, name=f"bank{h}_{c}") for c in range(PIECES)] for h in range(ROW_TILES)]
+
+        nc.scalar.copy(out=bias_rows[0:1, :], in_=bias_row[:])
+        turned = banks[1][PIECES - 1]
+        for h in range(ROW_TILES):
+            nc.tensor.transpose(turned[:, P * h : P * (h + 1)], bias_rows[:, h::ROW_TILES], identity[:])
 
         def group_x(copy, c, first, last):
             interleave(copy, x_grouped[c], x_raw[c], first, last)
@@ -144,6 +172,7 @@ def tile_picked_place_lin_bias_srt_l_kernel(tc, xT, w, b, gate, offs, out):
         quantize_x(0)
         group_w(nc.vector.tensor_copy, 0)
         group_w(nc.scalar.copy, 1)
+        nc.scalar.copy(out=bias[:], in_=turned[:, 0 : 2 * P : P])
         quantize_w(0)
         quantize_w(1)
         multiply(0)

@@ -20,8 +20,6 @@ SHARE = PIECE // 2
 PIECES = S // PIECE
 ROW_TILES = N // P
 CLEAR = 768
-STAGED = 2 * PIECE
-SHARED = 8
 QUADRANT = 32
 BANK = 512
 
@@ -45,9 +43,7 @@ def tile_picked_place_lin_bias_srt_l_kernel(tc, xT, w, b, gate, offs, out):
         offsets = keep.tile([P, S // 16], U16, name="offsets")
         gate_rows = keep.tile([P, S], F32, name="gate_rows")
         w_raw = keep.tile([P, PACK, N], F32, name="w_raw")
-        last = keep.tile([P, PACK * PIECE + STAGED - SHARED], F32, name="last")
-        x_raw = [keep.tile([P, PACK, PIECE], F32, name=f"x_raw{c}")[:] for c in range(PIECES - 1)]
-        x_raw.append(last[:, : PACK * PIECE].rearrange("p (j s) -> p j s", j=PACK))
+        x_raw = [keep.tile([P, PACK, PIECE], F32, name=f"x_raw{c}")[:] for c in range(PIECES)]
         windows = [keep.tile([P, T], F32, name=f"window{h}") for h in range(ROW_TILES)]
         bias = keep.tile([P, ROW_TILES], F32, name="bias")
         bias_row = keep.tile([1, N], F32, name="bias_row")
@@ -103,10 +99,10 @@ def tile_picked_place_lin_bias_srt_l_kernel(tc, xT, w, b, gate, offs, out):
         w_codes = [keep.tile([P, P], U32, name=f"w_codes{h}", align_bytes=64) for h in range(ROW_TILES)]
         w_scales = [keep.tile([P, P], U8, name=f"w_scales{h}", align_bytes=64) for h in range(ROW_TILES)]
         x_grouped = [keep.tile([P, PACK * PIECE], BF16, name=f"x_grouped{c}", align_bytes=64) for c in range(PIECES)]
-        x_codes = [keep.tile([P, PIECE], U32, name=f"x_codes{c}", tag=f"codes{c}", align_bytes=64) for c in range(PIECES)]
+        x_codes = [keep.tile([P, PIECE], U32, name=f"x_codes{c}", align_bytes=64) for c in range(PIECES)]
         x_scales = [keep.tile([P, PIECE], U8, name=f"x_scales{c}", align_bytes=64) for c in range(PIECES)]
         results = [keep.tile([P, S], F32, name=f"results{h}") for h in range(ROW_TILES)]
-        final = [last[:, PACK * PIECE - SHARED :], x_grouped[PIECES - 1][:].bitcast(F32)]
+        final = [[keep.tile([P, PIECE], F32, name=f"final{h}_{c}") for c in range(PIECES - 1)] for h in range(ROW_TILES)]
 
         banks = [[psum.tile([P, BANK], F32, name=f"bank{h}_{c}") for c in range(PIECES)] for h in range(ROW_TILES)]
 
@@ -165,8 +161,20 @@ def tile_picked_place_lin_bias_srt_l_kernel(tc, xT, w, b, gate, offs, out):
         def store(h, first, last, source):
             nc.sync.dma_start(out=out_rows[h, :, first:last], in_=source)
 
-        def stage(copy, h, first, last, place):
-            copy(out=place, in_=windows[h][:, first:last])
+        def leave(h, c):
+            first = PIECE * c
+            if c == PIECES - 1:
+                store(h, first, T, windows[h][:, first:])
+            else:
+                nc.gpsimd.tensor_scalar(
+                    out=final[h][c][:],
+                    in0=windows[h][:, first : first + PIECE],
+                    scalar1=1.0,
+                    scalar2=0.0,
+                    op0=mult,
+                    op1=add,
+                )
+                store(h, first, first + PIECE, final[h][c][:])
 
         group_x(nc.vector.tensor_copy, 0, 0, PIECE)
         quantize_x(0)
@@ -178,36 +186,20 @@ def tile_picked_place_lin_bias_srt_l_kernel(tc, xT, w, b, gate, offs, out):
         multiply(0)
         group_x(nc.scalar.copy, 1, 0, SHARE)
         group_x(nc.vector.tensor_copy, 1, SHARE, PIECE)
-        finish(0, 0)
-        scatter(0, 0)
-        quantize_x(1)
-        multiply(1)
-        finish(1, 0)
-        scatter(1, 0)
-        group_x(nc.vector.tensor_copy, 2, 0, PIECE)
-        finish(0, 1)
-        scatter(0, 1)
-        quantize_x(2)
-        multiply(2)
-        finish(1, 1)
-        scatter(1, 1)
-        group_x(nc.vector.tensor_copy, 3, 0, PIECE)
-        finish(0, 2)
-        stage(nc.vector.tensor_copy, 0, 0, STAGED, final[0])
-        store(0, 0, STAGED, final[0])
-        scatter(0, 2)
-        quantize_x(3)
-        multiply(3)
-        finish(1, 2)
-        stage(nc.vector.tensor_copy, 1, 0, PIECE, final[1][:, :PIECE])
-        stage(nc.scalar.copy, 1, PIECE, STAGED, final[1][:, PIECE:])
-        store(1, 0, STAGED, final[1])
-        finish(0, 3)
-        late = keep.tile([P, PIECE], F32, name="late", tag=f"codes{PIECES - 1}", align_bytes=64)
-        stage(nc.vector.tensor_copy, 0, STAGED, STAGED + PIECE, late[:])
-        store(0, STAGED, STAGED + PIECE, late[:])
-        scatter(0, 3)
-        store(0, STAGED + PIECE, T, windows[0][:, STAGED + PIECE :])
-        finish(1, 3)
-        nc.vector.tensor_copy(places(1, STAGED, S), results[1][:, STAGED:])
-        store(1, STAGED, T, windows[1][:, STAGED:])
+        for c in range(PIECES - 1):
+            finish(0, c)
+            scatter(0, c)
+            leave(0, c)
+            quantize_x(c + 1)
+            multiply(c + 1)
+            finish(1, c)
+            scatter(1, c)
+            leave(1, c)
+            if c + 2 < PIECES:
+                group_x(nc.vector.tensor_copy, c + 2, 0, PIECE)
+        finish(0, PIECES - 1)
+        scatter(0, PIECES - 1)
+        leave(0, PIECES - 1)
+        finish(1, PIECES - 1)
+        nc.vector.tensor_copy(places(1, S - PIECE, S), results[1][:, S - PIECE :])
+        leave(1, PIECES - 1)

@@ -99,10 +99,10 @@ def tile_picked_place_lin_bias_srt_l_kernel(tc, xT, w, b, gate, offs, out):
         w_codes = [keep.tile([P, P], U32, name=f"w_codes{h}", align_bytes=64) for h in range(ROW_TILES)]
         w_scales = [keep.tile([P, P], U8, name=f"w_scales{h}", align_bytes=64) for h in range(ROW_TILES)]
         x_grouped = [keep.tile([P, PACK * PIECE], BF16, name=f"x_grouped{c}", align_bytes=64) for c in range(PIECES)]
-        x_codes = [keep.tile([P, PIECE], U32, name=f"x_codes{c}", align_bytes=64) for c in range(PIECES)]
+        x_codes = [keep.tile([P, PIECE], U32, name=f"x_codes{c}", tag=f"codes{c}", align_bytes=64) for c in range(PIECES)]
         x_scales = [keep.tile([P, PIECE], U8, name=f"x_scales{c}", align_bytes=64) for c in range(PIECES)]
         results = [keep.tile([P, S], F32, name=f"results{h}") for h in range(ROW_TILES)]
-        final = [[keep.tile([P, PIECE], F32, name=f"final{h}_{c}") for c in range(PIECES - 1)] for h in range(ROW_TILES)]
+        final = [keep.tile([P, PIECE], F32, name=f"final{c}") for c in range(PIECES - 1)]
 
         banks = [[psum.tile([P, BANK], F32, name=f"bank{h}_{c}") for c in range(PIECES)] for h in range(ROW_TILES)]
 
@@ -161,20 +161,12 @@ def tile_picked_place_lin_bias_srt_l_kernel(tc, xT, w, b, gate, offs, out):
         def store(h, first, last, source):
             nc.sync.dma_start(out=out_rows[h, :, first:last], in_=source)
 
-        def leave(h, c):
-            first = PIECE * c
-            if c == PIECES - 1:
-                store(h, first, T, windows[h][:, first:])
-            else:
-                nc.gpsimd.tensor_scalar(
-                    out=final[h][c][:],
-                    in0=windows[h][:, first : first + PIECE],
-                    scalar1=1.0,
-                    scalar2=0.0,
-                    op0=mult,
-                    op1=add,
-                )
-                store(h, first, first + PIECE, final[h][c][:])
+        def pool_copy(out, in_):
+            nc.gpsimd.tensor_scalar(out=out, in0=in_, scalar1=1.0, scalar2=0.0, op0=mult, op1=add)
+
+        def leave(copy, h, first, last, place):
+            copy(out=place, in_=windows[h][:, first:last])
+            store(h, first, last, place)
 
         group_x(nc.vector.tensor_copy, 0, 0, PIECE)
         quantize_x(0)
@@ -189,17 +181,22 @@ def tile_picked_place_lin_bias_srt_l_kernel(tc, xT, w, b, gate, offs, out):
         for c in range(PIECES - 1):
             finish(0, c)
             scatter(0, c)
-            leave(0, c)
+            if c < 2:
+                leave(pool_copy, 0, PIECE * c, PIECE * (c + 1), final[c][:])
             quantize_x(c + 1)
             multiply(c + 1)
             finish(1, c)
+            if c == 2:
+                leave(nc.vector.tensor_copy, 1, 0, 2 * PIECE, x_grouped[3][:].bitcast(F32))
             scatter(1, c)
-            leave(1, c)
             if c + 2 < PIECES:
                 group_x(nc.vector.tensor_copy, c + 2, 0, PIECE)
-        finish(0, PIECES - 1)
-        scatter(0, PIECES - 1)
-        leave(0, PIECES - 1)
-        finish(1, PIECES - 1)
-        nc.vector.tensor_copy(places(1, S - PIECE, S), results[1][:, S - PIECE :])
-        leave(1, PIECES - 1)
+        leave(pool_copy, 1, 2 * PIECE, 3 * PIECE, final[2][:])
+        finish(0, 3)
+        late = keep.tile([P, PIECE], F32, name="late", tag="codes3", align_bytes=64)
+        leave(nc.vector.tensor_copy, 0, 2 * PIECE, 3 * PIECE, late[:])
+        finish(1, 3)
+        nc.vector.tensor_copy(places(0, 3 * PIECE, S), results[0][:, 3 * PIECE :])
+        store(0, 3 * PIECE, T, windows[0][:, 3 * PIECE :])
+        scatter(1, 3)
+        store(1, 3 * PIECE, T, windows[1][:, 3 * PIECE :])

@@ -102,7 +102,7 @@ def tile_picked_place_lin_bias_srt_l_kernel(tc, xT, w, b, gate, offs, out):
         x_codes = [keep.tile([P, PIECE], U32, name=f"x_codes{c}", tag=f"codes{c}", align_bytes=64) for c in range(PIECES)]
         x_scales = [keep.tile([P, PIECE], U8, name=f"x_scales{c}", align_bytes=64) for c in range(PIECES)]
         results = [keep.tile([P, S], F32, name=f"results{h}") for h in range(ROW_TILES)]
-        final = [keep.tile([P, PIECE], F32, name=f"final{c}") for c in range(PIECES - 1)]
+        final = keep.tile([P, PIECE], F32, name="final")
 
         banks = [[psum.tile([P, BANK], F32, name=f"bank{h}_{c}") for c in range(PIECES)] for h in range(ROW_TILES)]
 
@@ -161,9 +161,6 @@ def tile_picked_place_lin_bias_srt_l_kernel(tc, xT, w, b, gate, offs, out):
         def store(h, first, last, source):
             nc.sync.dma_start(out=out_rows[h, :, first:last], in_=source)
 
-        def pool_copy(out, in_):
-            nc.gpsimd.tensor_scalar(out=out, in0=in_, scalar1=1.0, scalar2=0.0, op0=mult, op1=add)
-
         def leave(copy, h, first, last, place):
             copy(out=place, in_=windows[h][:, first:last])
             store(h, first, last, place)
@@ -181,8 +178,6 @@ def tile_picked_place_lin_bias_srt_l_kernel(tc, xT, w, b, gate, offs, out):
         for c in range(PIECES - 1):
             finish(0, c)
             scatter(0, c)
-            if c < 2:
-                leave(pool_copy, 0, PIECE * c, PIECE * (c + 1), final[c][:])
             quantize_x(c + 1)
             multiply(c + 1)
             finish(1, c)
@@ -191,12 +186,12 @@ def tile_picked_place_lin_bias_srt_l_kernel(tc, xT, w, b, gate, offs, out):
             scatter(1, c)
             if c + 2 < PIECES:
                 group_x(nc.vector.tensor_copy, c + 2, 0, PIECE)
-        leave(pool_copy, 1, 2 * PIECE, 3 * PIECE, final[2][:])
         finish(0, 3)
-        late = keep.tile([P, PIECE], F32, name="late", tag="codes3", align_bytes=64)
-        leave(nc.vector.tensor_copy, 0, 2 * PIECE, 3 * PIECE, late[:])
+        late = keep.tile([P, 3 * PIECE], F32, name="late", tag="codes3", align_bytes=64)
+        leave(nc.vector.tensor_copy, 0, 0, 3 * PIECE, late[:])
         finish(1, 3)
-        nc.vector.tensor_copy(places(0, 3 * PIECE, S), results[0][:, 3 * PIECE :])
+        leave(nc.vector.tensor_copy, 1, 2 * PIECE, 3 * PIECE, final[:])
+        scatter(0, 3)
         store(0, 3 * PIECE, T, windows[0][:, 3 * PIECE :])
-        scatter(1, 3)
+        nc.vector.tensor_copy(places(1, 3 * PIECE, S), results[1][:, 3 * PIECE :])
         store(1, 3 * PIECE, T, windows[1][:, 3 * PIECE :])

@@ -71,7 +71,7 @@ def tile_picked_place_lin_bias_srt_l_kernel(tc, xT, w, b, gate, offs, out):
         )
 
         x_rows = xT.rearrange("(p j) s -> p j s", j=PACK)
-        out_rows = out.rearrange("(p h) t -> h p t", h=ROW_TILES)
+        out_rows = out.rearrange("(h p) t -> h p t", h=ROW_TILES)
 
         def load_x(c):
             nc.sync.dma_start(out=x_raw[c], in_=x_rows[:, :, PIECE * c : PIECE * (c + 1)])
@@ -109,13 +109,13 @@ def tile_picked_place_lin_bias_srt_l_kernel(tc, xT, w, b, gate, offs, out):
         nc.scalar.copy(out=bias_rows[0:1, :], in_=bias_row[:])
         turned = banks[1][PIECES - 1]
         for h in range(ROW_TILES):
-            nc.tensor.transpose(turned[:, P * h : P * (h + 1)], bias_rows[:, h::ROW_TILES], identity[:])
+            nc.tensor.transpose(turned[:, P * h : P * (h + 1)], bias_rows[:, P * h : P * (h + 1)], identity[:])
 
         def group_x(copy, c, first, last):
             interleave(copy, x_grouped[c], x_raw[c], first, last)
 
         def group_w(copy, h):
-            columns = w_raw[:].rearrange("p j (i h) -> p j h i", h=ROW_TILES)[:, :, h, :]
+            columns = w_raw[:, :, P * h : P * (h + 1)]
             interleave(copy, w_grouped[:, PACK * P * h : PACK * P * (h + 1)], columns, 0, P)
 
         def quantize_w(h):

@@ -88,8 +88,7 @@ def tile_picked_place_lin_bias_srt_l_kernel(tc, xT, w, b, gate, offs, out):
         load_x(2)
         load_gate(PIECE, 2 * PIECE)
         load_x(3)
-        load_gate(2 * PIECE, 3 * PIECE)
-        load_gate(3 * PIECE, S)
+        load_gate(2 * PIECE, S)
 
         for h, first, end in ((0, 0, T // 2), (0, T // 2, T), (1, 0, CLEAR)):
             nc.vector.tensor_copy(out=windows[h][:, first:end], in_=zero[:].to_broadcast([P, end - first]))
@@ -188,7 +187,8 @@ def tile_picked_place_lin_bias_srt_l_kernel(tc, xT, w, b, gate, offs, out):
                 group_x(nc.vector.tensor_copy, c + 2, 0, PIECE)
         finish(0, 3)
         late = keep.tile([P, 3 * PIECE], F32, name="late", tag="codes3", align_bytes=64)
-        leave(nc.vector.tensor_copy, 0, 0, 3 * PIECE, late[:])
+        leave(nc.vector.tensor_copy, 0, 0, PIECE, late[:, :PIECE])
+        leave(nc.vector.tensor_copy, 0, PIECE, 3 * PIECE, late[:, PIECE:])
         finish(1, 3)
         leave(nc.vector.tensor_copy, 1, 2 * PIECE, 3 * PIECE, final[:])
         scatter(0, 3)

@@ -26,8 +26,8 @@ BANK = 512
 
 def interleave(copy, grouped, raw, first, last):
     copy(
-        out=grouped[:, PACK * first : PACK * last].rearrange("p (c i j) -> p c j i", i=4, j=PACK),
-        in_=raw[:, :, first:last].rearrange("p j (c i) -> p c j i", i=4),
+        out=grouped[:, PACK * first : PACK * last].rearrange("p (c i j) -> p c j i", i=2, j=PACK),
+        in_=raw[:, :, first:last].rearrange("p j (c i) -> p c j i", i=2),
     )
 
 

from contextlib import ExitStack

import concourse.mybir as mybir

K, T, S, N = 512, 2048, 1024, 256
FLOPS = 2 * K * N * S
BYTES = 4 * (K * S + K * N + N + S + N * T) + 2 * 128 * (S // 16)

F32 = mybir.dt.float32
BF16 = mybir.dt.bfloat16
U32 = mybir.dt.uint32
U16 = mybir.dt.uint16
U8 = mybir.dt.uint8
FP8X4 = mybir.dt.float8_e4m3fn_x4

P = 128
PACK = 4
PIECE = 256
SHARE = PIECE // 2
PIECES = S // PIECE
ROW_TILES = N // P
CLEAR = 768
QUADRANT = 32
BANK = 512


def interleave(copy, grouped, raw, first, last):
    copy(
        out=grouped[:, PACK * first : PACK * last].rearrange("p (c i j) -> p c j i", i=2, j=PACK),
        in_=raw[:, :, first:last].rearrange("p j (c i) -> p c j i", i=2),
    )


def tile_picked_place_lin_bias_srt_l_kernel(tc, xT, w, b, gate, offs, out):
    nc = tc.nc
    add, mult = mybir.AluOpType.add, mybir.AluOpType.mult
    plain = mybir.ActivationFunctionType.Copy

    with ExitStack() as ctx:
        keep = ctx.enter_context(tc.tile_pool(name="keep", bufs=1))
        psum = ctx.enter_context(tc.psum_pool(name="psum", bufs=1))

        offsets = keep.tile([P, S // 16], U16, name="offsets")
        gate_rows = keep.tile([P, S], F32, name="gate_rows")
        w_raw = keep.tile([P, PACK, N], F32, name="w_raw")
        x_raw = [keep.tile([P, PACK, PIECE], F32, name=f"x_raw{c}")[:] for c in range(PIECES)]
        windows = [keep.tile([P, T], F32, name=f"window{h}") for h in range(ROW_TILES)]
        bias = keep.tile([P, ROW_TILES], F32, name="bias")
        bias_row = keep.tile([1, N], F32, name="bias_row")
        bias_rows = keep.tile([P, N], F32, name="bias_rows")
        zero = keep.tile([P, 1], F32, name="zero")
        ones = keep.tile([P, P], F32, name="ones")
        column = keep.tile([P, P], F32, name="column", align_bytes=64)
        row = keep.tile([P, QUADRANT], F32, name="row", align_bytes=64)
        number = keep.tile([P, 1], F32, name="number")
        identity = keep.tile([P, P], F32, name="identity")
        nc.gpsimd.memset(zero[:], 0.0)
        nc.gpsimd.memset(ones[:], 1.0)
        for first in range(0, P, QUADRANT):
            nc.gpsimd.memset(number[first : first + QUADRANT, :], float(first))
        nc.gpsimd.memset(bias_rows[:], 0.0)
        nc.vector.tensor_tensor_scan(column[:], ones[:], ones[:], 0.0, mult, add)
        nc.vector.transpose(row[:], column[:, :QUADRANT])
        nc.vector.tensor_scalar(
            out=identity[:],
            in0=column[:],
            scalar1=row[:, 0:1],
            scalar2=number[:],
            op0=mybir.AluOpType.subtract,
            op1=mybir.AluOpType.is_equal,
        )

        x_rows = xT.rearrange("(p j) s -> p j s", j=PACK)
        out_rows = out.rearrange("(h p) t -> h p t", h=ROW_TILES)

        def load_x(c):
            nc.sync.dma_start(out=x_raw[c], in_=x_rows[:, :, PIECE * c : PIECE * (c + 1)])

        def load_gate(first, last):
            nc.sync.dma_start(out=gate_rows[:, first:last], in_=gate[0:P, first:last])

        load_x(0)
        nc.sync.dma_start(out=bias_row[:], in_=b.rearrange("m o -> o m"))
        nc.sync.dma_start(out=w_raw[:], in_=w.rearrange("(p j) m -> p j m", j=PACK))
        load_x(1)
        load_gate(0, PIECE)
        nc.sync.dma_start(offsets[:], offs)
        load_x(2)
        load_gate(PIECE, 2 * PIECE)
        load_x(3)
        load_gate(2 * PIECE, S)

        for h, first, end in ((0, 0, T // 2), (0, T // 2, T), (1, 0, CLEAR)):
            nc.vector.tensor_copy(out=windows[h][:, first:end], in_=zero[:].to_broadcast([P, end - first]))
        nc.scalar.copy(out=windows[1][:, CLEAR:], in_=zero[:].to_broadcast([P, T - CLEAR]))

        w_grouped = keep.tile([P, PACK * N], BF16, name="w_grouped", align_bytes=64)
        w_codes = [keep.tile([P, P], U32, name=f"w_codes{h}", align_bytes=64) for h in range(ROW_TILES)]
        w_scales = [keep.tile([P, P], U8, name=f"w_scales{h}", align_bytes=64) for h in range(ROW_TILES)]
        x_grouped = [keep.tile([P, PACK * PIECE], BF16, name=f"x_grouped{c}", align_bytes=64) for c in range(PIECES)]
        x_codes = [keep.tile([P, PIECE], U32, name=f"x_codes{c}", tag=f"codes{c}", align_bytes=64) for c in range(PIECES)]
        x_scales = [keep.tile([P, PIECE], U8, name=f"x_scales{c}", align_bytes=64) for c in range(PIECES)]
        results = [keep.tile([P, S], F32, name=f"results{h}") for h in range(ROW_TILES)]
        final = keep.tile([P, PIECE], F32, name="final")

        banks = [[psum.tile([P, BANK], F32, name=f"bank{h}_{c}") for c in range(PIECES)] for h in range(ROW_TILES)]

        nc.scalar.copy(out=bias_rows[0:1, :], in_=bias_row[:])
        turned = banks[1][PIECES - 1]
        for h in range(ROW_TILES):
            nc.tensor.transpose(turned[:, P * h : P * (h + 1)], bias_rows[:, P * h : P * (h + 1)], identity[:])

        def group_x(copy, c, first, last):
            interleave(copy, x_grouped[c], x_raw[c], first, last)

        def group_w(copy, h):
            columns = w_raw[:, :, P * h : P * (h + 1)]
            interleave(copy, w_grouped[:, PACK * P * h : PACK * P * (h + 1)], columns, 0, P)

        def quantize_w(h):
            nc.vector.quantize_mx(
                out=w_codes[h][:].bitcast(FP8X4),
                scales=w_scales[h][:],
                in_=w_grouped[:, PACK * P * h : PACK * P * (h + 1)],
            )

        def quantize_x(c):
            nc.vector.quantize_mx(out=x_codes[c][:].bitcast(FP8X4), scales=x_scales[c][:], in_=x_grouped[c][:])

        def multiply(c):
            for h in range(ROW_TILES):
                nc.tensor.matmul_mx(
                    out=banks[h][c][:, :PIECE],
                    lhsT=w_codes[h][:].bitcast(FP8X4),
                    lhsT_scale=w_scales[h][:],
                    rhs=x_codes[c][:].bitcast(FP8X4),
                    rhs_scale=x_scales[c][:],
                    start=True,
                    stop=True,
                )

        def finish(h, c):
            columns = slice(PIECE * c, PIECE * (c + 1))
            nc.vector.scalar_tensor_tensor(
                out=results[h][:, columns],
                in0=banks[h][c][:, :PIECE],
                scalar=bias[:, h : h + 1],
                in1=gate_rows[:, columns],
                op0=add,
                op1=mult,
            )

        def places(h, first, last):
            return windows[h][:].indirect(offsets[:, first // 16 : last // 16])

        def scatter(h, c):
            first, last = PIECE * c, PIECE * (c + 1)
            nc.scalar.activation(places(h, first, last), results[h][:, first:last], plain)

        def store(h, first, last, source):
            nc.sync.dma_start(out=out_rows[h, :, first:last], in_=source)

        def leave(copy, h, first, last, place):
            copy(out=place, in_=windows[h][:, first:last])
            store(h, first, last, place)

        group_x(nc.vector.tensor_copy, 0, 0, PIECE)
        quantize_x(0)
        group_w(nc.vector.tensor_copy, 0)
        group_w(nc.scalar.copy, 1)
        nc.scalar.copy(out=bias[:], in_=turned[:, 0 : 2 * P : P])
        quantize_w(0)
        quantize_w(1)
        multiply(0)
        group_x(nc.scalar.copy, 1, 0, SHARE)
        group_x(nc.vector.tensor_copy, 1, SHARE, PIECE)
        for c in range(PIECES - 1):
            finish(0, c)
            scatter(0, c)
            quantize_x(c + 1)
            multiply(c + 1)
            finish(1, c)
            if c == 2:
                leave(nc.vector.tensor_copy, 1, 0, 2 * PIECE, x_grouped[3][:].bitcast(F32))
            scatter(1, c)
            if c + 2 < PIECES:
                group_x(nc.vector.tensor_copy, c + 2, 0, PIECE)
        finish(0, 3)
        late = keep.tile([P, 3 * PIECE], F32, name="late", tag="codes3", align_bytes=64)
        leave(nc.vector.tensor_copy, 0, 0, PIECE, late[:, :PIECE])
        leave(nc.vector.tensor_copy, 0, PIECE, 3 * PIECE, late[:, PIECE:])
        finish(1, 3)
        leave(nc.vector.tensor_copy, 1, 2 * PIECE, 3 * PIECE, final[:])
        scatter(0, 3)
        store(0, 3 * PIECE, T, windows[0][:, 3 * PIECE :])
        nc.vector.tensor_copy(places(1, 3 * PIECE, S), results[1][:, 3 * PIECE :])
        store(1, 3 * PIECE, T, windows[1][:, 3 * PIECE :])
